import numpy as np
import ml_dtypes


def mxq(x, axis, fmt="e4m3"):
    dtype, down = {"e4m3": (ml_dtypes.float8_e4m3fn, 7), "e5m2": (ml_dtypes.float8_e5m2, 14)}[fmt]
    v = np.moveaxis(np.asarray(x, np.float32).astype(ml_dtypes.bfloat16).astype(np.float64), axis, -1)
    blocks = v.reshape(v.shape[:-1] + (-1, 32))
    amax = np.abs(blocks).max(-1, keepdims=True)
    byte = np.maximum(np.where(amax > 0, np.frexp(amax)[1] - 1 + 127, 0) - down, 1)
    scale = np.exp2(byte - 127.0)
    codes = (blocks / scale).astype(np.float32).astype(dtype).astype(np.float64)
    return np.moveaxis((codes * scale).reshape(v.shape), -1, axis)


WIDE = False


def mx_kscale(k):
    if not WIDE:
        return np.ones(k)
    levels = np.array([10, -10, 5, -5, 0])
    if k % 512:
        return np.exp2(np.random.permutation(np.resize(levels, k // 32))).repeat(32)
    a = np.empty((k // 512, 16))
    for p in range(k // 512):
        a[p, :8] = np.random.permutation(np.resize(levels, 8))
        for g in range(8):
            far = levels[np.abs(levels - a[p, g]) >= 10]
            a[p, g + 8] = far[np.random.randint(len(far))]
    return np.exp2(a.ravel()).repeat(32)


def f64(x):
    return np.asarray(x).astype(np.float64)


def striped(idx):
    return np.tile(idx.reshape(-1, 16).T, (8, 1)).astype(np.uint16)


def unstriped(offs):
    return offs[:16].T.reshape(-1).astype(np.int64)


E2M1 = np.array([0.0, 0.5, 1.0, 1.5, 2.0, 3.0, 4.0, 6.0, -0.0, -0.5, -1.0, -1.5, -2.0, -3.0, -4.0, -6.0])


def pack_weight(w, fmt):
    k, n = w.shape
    w = f64(np.asarray(w, np.float32).astype(ml_dtypes.bfloat16)).reshape(k // 32, 32, n)
    amax = np.abs(w).max(1)
    if fmt == "e4m3":
        byte = np.frexp(amax)[1] - 1 + 127 - 7
    else:
        mant, ex = np.frexp(amax / 6.0)
        byte = np.where(mant > 0.5, ex, ex - 1) + 127
    byte = np.clip(np.where(amax > 0, byte, 1), 1, 254)
    scaled = (w * np.exp2(127.0 - byte)[:, None, :]).reshape(k, n).astype(np.float32)
    by_word = np.ascontiguousarray(scaled.reshape(k // 512, 128, 4, n).transpose(0, 1, 3, 2))
    if fmt == "e4m3":
        words = by_word.astype(ml_dtypes.float8_e4m3fn).view(np.uint8)
    else:
        c = by_word.astype(ml_dtypes.float4_e2m1fn).view(np.uint8) & 0xF
        words = (c[..., 0::2] | (c[..., 1::2] << 4)).reshape(k // 512, 128, 2 * n)
    return np.ascontiguousarray(words), np.ascontiguousarray(byte.astype(np.uint8).reshape(k // 512, 16, n))


def unpack_weight(words, scales, fmt):
    g, _, n = scales.shape
    words = np.ascontiguousarray(words).reshape(g, 128, n, -1)
    if fmt == "e4m3":
        vals = words.view(ml_dtypes.float8_e4m3fn).astype(np.float64)
    else:
        nib = np.empty((g, 128, n, 4), np.uint8)
        nib[..., 0::2] = words & 0xF
        nib[..., 1::2] = words >> 4
        vals = E2M1[nib]
    vals = vals * np.repeat(np.exp2(scales.astype(np.float64) - 127.0), 8, axis=1)[..., None]
    return vals.transpose(0, 1, 3, 2).reshape(g * 512, n)


def relu(v):
    return np.maximum(v, 0.0)


K, T, E, C, H, N = 512, 640, 4, 128, 512, 256


def by_expert(wq, xq):
    return np.concatenate([wq[e].T @ xq[:, e * C:(e + 1) * C] for e in range(E)], axis=1)


def setup_inputs():
    n = np.random.standard_normal
    s = mx_kscale(K)[:, None]
    u = mx_kscale(H)
    w1 = [pack_weight(m, "e2m1") for m in n((E + 1, K, H)) / np.sqrt(K) / s[None]]
    w3 = [pack_weight(m, "e2m1") for m in n((E + 1, K, H)) / np.sqrt(K) / s[None] * u[None, None, :]]
    w2 = [pack_weight(m, "e2m1") for m in n((E + 1, H, N)) / np.sqrt(H) / u[None, :, None]]
    return {
        "xT": (n((K, T)) * s).astype(np.float32),
        "w1_words": np.stack([m[0] for m in w1]),
        "w1_scales": np.stack([m[1] for m in w1]),
        "w3_words": np.stack([m[0] for m in w3]),
        "w3_scales": np.stack([m[1] for m in w3]),
        "w2_words": np.stack([m[0] for m in w2]),
        "w2_scales": np.stack([m[1] for m in w2]),
        "gate": np.tile(np.random.uniform(0.2, 1.0, E * C), (N, 1)).astype(np.float32),
        "offs": striped(np.random.permutation(T)[:E * C]),
    }


def reference(xT, w1_words, w1_scales, w3_words, w3_scales, w2_words, w2_scales, gate, offs):
    idx = unstriped(offs)
    w1 = np.stack([unpack_weight(w1_words[e], w1_scales[e], "e2m1") for e in range(E + 1)])
    w3 = np.stack([unpack_weight(w3_words[e], w3_scales[e], "e2m1") for e in range(E + 1)])
    w2 = np.stack([unpack_weight(w2_words[e], w2_scales[e], "e2m1") for e in range(E + 1)])
    w1q, w3q, w2q = w1, w3, w2
    xs = mxq(f64(xT), 0, "e4m3")
    hs = relu(w1q[E].T @ xs) * (w3q[E].T @ xs)
    ys = w2q[E].T @ mxq(hs, 0, "e4m3")
    xq = mxq(f64(xT)[:, idx], 0, "e4m3")
    h = relu(by_expert(w1q, xq))
    h = h * by_expert(w3q, xq)
    y = by_expert(w2q, mxq(h, 0, "e4m3"))
    out = ys
    out[:, idx] += f64(gate) * y
    return out

@@ -1,0 +1,297 @@
+from contextlib import ExitStack
+
+import concourse.mybir as mybir
+from concourse.masks import make_identity
+
+FLOPS = 1509949440
+
+K, T, E, C, H, N = 512, 640, 4, 128, 512, 256
+S = E * C
+SHARED = E
+P = 128
+HALVES = N // P
+
+F32 = mybir.dt.float32
+BF16 = mybir.dt.bfloat16
+I32 = mybir.dt.int32
+U32 = mybir.dt.uint32
+U16 = mybir.dt.uint16
+U8 = mybir.dt.uint8
+FP8X4 = mybir.dt.float8_e4m3fn_x4
+FP4X4 = mybir.dt.float4_e2m1fn_x4
+RELU = mybir.ActivationFunctionType.Relu
+MULT = mybir.AluOpType.mult
+ADD = mybir.AluOpType.add
+
+X_SPLIT = 256
+
+
+def tile_moe_shr_glu_relu_kernel(
+    tc, xT, w1_words, w1_scales, w3_words, w3_scales, w2_words, w2_scales, gate, offs, out
+):
+    nc = tc.nc
+    with ExitStack() as ctx:
+        keep = ctx.enter_context(tc.tile_pool(name="keep", bufs=1))
+        work = ctx.enter_context(tc.tile_pool(name="work", bufs=6))
+        psum = ctx.enter_context(tc.psum_pool(name="psum", bufs=2))
+
+        offsets = keep.tile([P, S // 16], U16, name="offsets")
+        x_a = keep.tile([P, 4, X_SPLIT], F32, name="x_a")
+        x_b = keep.tile([P, 4, T - X_SPLIT], F32, name="x_b")
+        w1 = keep.tile([P, E + 1, 2 * H], U8, name="w1", align_bytes=64)
+        w3 = keep.tile([P, E + 1, 2 * H], U8, name="w3", align_bytes=64)
+        w2 = keep.tile([P, E + 1, 2 * N], U8, name="w2", align_bytes=64)
+        s1 = keep.tile([P, E + 1, H], U8, name="s1", align_bytes=64)
+        s3 = keep.tile([P, E + 1, H], U8, name="s3", align_bytes=64)
+        s2 = keep.tile([P, E + 1, N], U8, name="s2", align_bytes=64)
+        gates = keep.tile([P, HALVES, S], F32, name="gates")
+        ident = keep.tile([P, P], F32, name="ident")
+        warm = keep.tile([P, 1], F32, name="warm")
+        pairs = [keep.tile([P, T], U32, name=f"pairs{u}") for u in range(2)]
+        x_in = keep.tile([P, T, 4], BF16, name="x_in", align_bytes=64)
+        x_codes = keep.tile([P, T], U32, name="x_codes", align_bytes=64)
+        x_scales = keep.tile([P, T], U8, name="x_scales", align_bytes=64)
+        g_codes = keep.tile([P, S], U32, name="g_codes", align_bytes=64)
+        g_scales = keep.tile([P, S], U8, name="g_scales", align_bytes=64)
+        hs_codes = keep.tile([P, T], U32, name="hs_codes", align_bytes=64)
+        hs_scales = keep.tile([P, T], U8, name="hs_scales", align_bytes=64)
+        windows = [keep.tile([P, T], F32, name=f"window{h}") for h in range(HALVES)]
+        results = [keep.tile([P, T], F32, name=f"result{h}") for h in range(HALVES)]
+
+        x_rows = xT.rearrange("(p j) t -> p j t", j=4)
+
+        def load_words(eng, tile, words, e0, e1):
+            eng.dma_start(
+                out=tile[:, e0:e1, :].bitcast(I32),
+                in_=words[e0:e1, 0].rearrange("e p b -> p e b").bitcast(I32),
+            )
+
+        def load_scales(eng, tile, scales, r):
+            rows = scales[:, 0].rearrange("e (q r) c -> r q e c", r=4)
+            eng.dma_start(out=tile[r:P:32, :, :].bitcast(I32), in_=rows[r].bitcast(I32))
+
+        def zero_plane(eng, tile):
+            eng.memset(tile[:].rearrange("p e c -> p (e c)").bitcast(I32), 0)
+
+        def touch(words):
+            nc.gpsimd.memset(words.bitcast(I32), 0)
+
+        nc.sync.dma_start(out=x_a[:], in_=x_rows[:, :, :X_SPLIT])
+        load_words(nc.sync, w1, w1_words, SHARED, SHARED + 1)
+        nc.sync.dma_start(offsets[:], offs)
+        zero_plane(nc.gpsimd, s1)
+        for r in range(4):
+            load_scales(nc.sync, s1, w1_scales, r)
+        touch(x_b[:, 0, 0:1])
+        nc.sync.dma_start(out=x_b[:], in_=x_rows[:, :, X_SPLIT:])
+        touch(w3[:, SHARED, 0:4])
+        load_words(nc.sync, w3, w3_words, SHARED, SHARED + 1)
+        zero_plane(nc.gpsimd, s3)
+        for r in range(4):
+            load_scales(nc.sync, s3, w3_scales, r)
+        touch(w1[:, 0, 0:4])
+        load_words(nc.sync, w1, w1_words, 0, E)
+        touch(w3[:, 0, 0:4])
+        load_words(nc.sync, w3, w3_words, 0, E)
+        zero_plane(nc.gpsimd, s2)
+        for r in range(4):
+            load_scales(nc.sync, s2, w2_scales, r)
+        touch(w2[:, 0, 0:4])
+        load_words(nc.sync, w2, w2_words, 0, E + 1)
+        touch(gates[:, 0, 0:1])
+        nc.sync.dma_start(out=gates[:], in_=gate.rearrange("(h p) s -> p h s", p=P))
+        make_identity(nc, ident[:])
+        nc.vector.memset(warm[:], 0.0)
+        nc.scalar.activation(warm[:], warm[:], RELU)
+        for h in range(HALVES):
+            nc.vector.memset(windows[h][:], 0.0)
+
+        def x_part(t0, t1):
+            return x_a[:, :, t0:t1] if t1 <= X_SPLIT else x_b[:, :, t0 - X_SPLIT : t1 - X_SPLIT]
+
+        def lay_shared(eng_copy, t0, t1):
+            eng_copy(out=x_in[:, t0:t1, :], in_=x_part(t0, t1).rearrange("p j t -> p t j"))
+
+        def quantize_shared(t0, t1):
+            nc.vector.quantize_mx(
+                out=x_codes[:, t0:t1].bitcast(FP8X4),
+                scales=x_scales[:, t0:t1],
+                in_=x_in[:, t0:t1, :].rearrange("p t j -> p (t j)"),
+            )
+
+        def cast_pairs(copy, u, t0, t1):
+            copy(
+                out=pairs[u][:, t0:t1].bitcast(BF16).rearrange("p (t d) -> p t d", d=2),
+                in_=x_part(t0, t1)[:, 2 * u : 2 * u + 2, :].rearrange("p d t -> p t d"),
+            )
+
+        def gather(j0, j1):
+            grouped = work.tile([P, j1 - j0, 2], U32, name="grouped", align_bytes=64)
+            for u in range(2):
+                nc.vector.tensor_copy(
+                    out=grouped[:, :, u], in_=pairs[u][:].indirect(offsets[:, j0 // 16 : j1 // 16])
+                )
+            nc.vector.quantize_mx(
+                out=g_codes[:, j0:j1].bitcast(FP8X4),
+                scales=g_scales[:, j0:j1],
+                in_=grouped[:].rearrange("p s u -> p (s u)").bitcast(BF16),
+            )
+
+        def first_product(codes, scales, cols, words, planes, e, tag, bufs):
+            bank = psum.tile([P, H], F32, name="bank_" + tag, tag=tag, bufs=bufs)
+            nc.tensor.matmul_mx(
+                out=bank[:],
+                lhsT=codes[:, cols].bitcast(FP8X4),
+                lhsT_scale=scales[:, cols],
+                rhs=words[:, e, :].bitcast(FP4X4),
+                rhs_scale=planes[:, e, :],
+                start=True,
+                stop=True,
+            )
+            return bank
+
+        def relu_side(e, codes, scales, cols):
+            bank = first_product(codes, scales, cols, w1, s1, e, "a", 2)
+            positive = work.tile([P, H], F32, name="positive", bufs=9)
+            nc.scalar.activation(positive[:], bank[:], RELU)
+            return positive
+
+        def factor_side(e, codes, scales, cols, positive):
+            bank = first_product(codes, scales, cols, w3, s3, e, "b", 3)
+            hidden = work.tile([P, H], BF16, name="hidden", align_bytes=64)
+            nc.vector.tensor_tensor(hidden[:], bank[:], positive[:], MULT)
+            return hidden
+
+        def turn(group):
+            n = len(group)
+            bank = psum.tile([P, n, 2, P], F32, name="bank_t", tag="t")
+            for i, hidden in enumerate(group):
+                words = hidden[:].bitcast(F32)
+                for u in range(2):
+                    nc.tensor.transpose(bank[:, i, u, :], words[:, u::2], ident[:])
+            turned = work.tile([P, n, P, 2], F32, name="turned", align_bytes=64)
+            nc.scalar.copy(out=turned[:], in_=bank[:].rearrange("p i u r -> p i r u"))
+            return turned
+
+        def quantize_hidden(turned, codes, scales):
+            nc.vector.quantize_mx(
+                out=codes.bitcast(FP8X4),
+                scales=scales,
+                in_=turned[:].rearrange("p i r u -> p (i r u)").bitcast(BF16),
+            )
+
+        def layer2(e, h, bank, codes, scales):
+            nc.tensor.matmul_mx(
+                out=bank,
+                lhsT=w2[:, e, 2 * P * h : 2 * P * (h + 1)].bitcast(FP4X4),
+                lhsT_scale=s2[:, e, P * h : P * (h + 1)],
+                rhs=codes.bitcast(FP8X4),
+                rhs_scale=scales,
+                start=True,
+                stop=True,
+            )
+
+        def experts_out(e0, n, turned):
+            codes = work.tile([P, n, C], U32, name="h_codes", align_bytes=64)
+            scales = work.tile([P, n, C], U8, name="h_scales", align_bytes=64)
+            quantize_hidden(turned, codes[:].rearrange("p n c -> p (n c)"), scales[:].rearrange("p n c -> p (n c)"))
+            bank = psum.tile([P, HALVES, n * C], F32, name="bank_y", tag="y", bufs=1)
+            for i in range(n):
+                for h in range(HALVES):
+                    layer2(e0 + i, h, bank[:, h, i * C : (i + 1) * C], codes[:, i, :], scales[:, i, :])
+            y = work.tile([P, HALVES, n * C], F32, name="y")
+            nc.scalar.copy(out=y[:], in_=bank[:])
+            return y
+
+        def scatter(e0, n, h, y):
+            nc.vector.tensor_tensor(
+                windows[h][:].indirect(offsets[:, e0 * C // 16 : (e0 + n) * C // 16]),
+                y[:, h, :],
+                gates[:, h, e0 * C : (e0 + n) * C],
+                MULT,
+            )
+
+        def cols(i, n=1):
+            return slice(i * P, (i + n) * P)
+
+        chunks = T // P
+        groups = [(0, 2), (2, 2), (4, 1), (5, 2), (7, 2)]
+        hidden = {}
+        turned = {}
+        ys = {}
+        total = chunks + E
+
+        positive = {}
+
+        def where(c):
+            if c < chunks:
+                return SHARED, x_codes, x_scales, cols(c)
+            return c - chunks, g_codes, g_scales, cols(c - chunks)
+
+        def a_step(c):
+            positive[c] = relu_side(*where(c))
+
+        def b_step(c):
+            hidden[c] = factor_side(*where(c), positive[c])
+
+        def finish(g):
+            c, n = groups[g]
+            if c < chunks:
+                quantize_hidden(turned[g], hs_codes[:, cols(c, n)], hs_scales[:, cols(c, n)])
+            else:
+                ys[g] = experts_out(c - chunks, n, turned[g])
+
+        lay_shared(nc.vector.tensor_copy, 0, 128)
+        lay_shared(nc.vector.tensor_copy, 128, 256)
+        quantize_shared(0, 128)
+        quantize_shared(128, 256)
+        cast_pairs(nc.vector.tensor_copy, 0, 0, 256)
+        cast_pairs(nc.vector.tensor_copy, 1, 0, 256)
+        cast_pairs(nc.vector.tensor_copy, 0, 256, 640)
+        cast_pairs(nc.vector.tensor_copy, 1, 256, 640)
+        a_step(0)
+        a_step(1)
+        lay_shared(nc.vector.tensor_copy, 256, 640)
+        quantize_shared(256, 512)
+        quantize_shared(512, 640)
+        gather(0, 256)
+        gather(256, 512)
+        a_step(2)
+        a_step(3)
+        a_step(4)
+        b_step(0)
+        b_step(1)
+        a_step(5)
+        b_step(5)
+        a_step(6)
+        b_step(6)
+        turned[0] = turn([hidden[0], hidden[1]])
+        a_step(7)
+        b_step(7)
+        turned[3] = turn([hidden[5], hidden[6]])
+        a_step(8)
+        b_step(8)
+        finish(0)
+        finish(3)
+        turned[4] = turn([hidden[7], hidden[8]])
+        b_step(2)
+        finish(4)
+        b_step(3)
+        turned[1] = turn([hidden[2], hidden[3]])
+        b_step(4)
+        turned[2] = turn([hidden[4]])
+        finish(1)
+        finish(2)
+        tail = psum.tile([P, HALVES, P], F32, name="bank_tail", tag="a")
+        bodies = []
+        for h in range(HALVES):
+            body = psum.tile([P, 512], F32, name="bank_body", tag="b", bufs=3)
+            layer2(SHARED, h, body[:], hs_codes[:, 0:512], hs_scales[:, 0:512])
+            layer2(SHARED, h, tail[:, h, :], hs_codes[:, 512:640], hs_scales[:, 512:640])
+            bodies.append(body)
+        for h in range(HALVES):
+            scatter(0, 2, h, ys[3])
+            scatter(2, 2, h, ys[4])
+            for bank, t0, t1 in ((bodies[h][:], 0, 512), (tail[:, h, :], 512, 640)):
+                nc.vector.tensor_tensor(results[h][:, t0:t1], bank, windows[h][:, t0:t1], ADD)
+                nc.sync.dma_start(out=out[h * P : (h + 1) * P, t0:t1], in_=results[h][:, t0:t1])

@@ -36,109 +36,70 @@ def tile_moe_shr_glu_relu_kernel(
         psum = ctx.enter_context(tc.psum_pool(name="psum", bufs=2))
 
         offsets = keep.tile([P, S // 16], U16, name="offsets")
-        x_a = keep.tile([P, 4, X_SPLIT], F32, name="x_a")
-        x_b = keep.tile([P, 4, T - X_SPLIT], F32, name="x_b")
+        x_low = keep.tile([P, 2, T], F32, name="x_low", tag="x_low", align_bytes=64)
+        x_high = [keep.tile([P, 2, n], F32, name=f"x_high{n}") for n in (X_SPLIT, T - X_SPLIT)]
         w1 = keep.tile([P, E + 1, 2 * H], U8, name="w1", align_bytes=64)
-        w3 = keep.tile([P, E + 1, 2 * H], U8, name="w3", align_bytes=64)
-        w2 = keep.tile([P, E + 1, 2 * N], U8, name="w2", align_bytes=64)
         s1 = keep.tile([P, E + 1, H], U8, name="s1", align_bytes=64)
         s3 = keep.tile([P, E + 1, H], U8, name="s3", align_bytes=64)
-        s2 = keep.tile([P, E + 1, N], U8, name="s2", align_bytes=64)
-        gates = keep.tile([P, HALVES, S], F32, name="gates")
         ident = keep.tile([P, P], F32, name="ident")
-        warm = keep.tile([P, 1], F32, name="warm")
-        pairs = [keep.tile([P, T], U32, name=f"pairs{u}") for u in range(2)]
-        x_in = keep.tile([P, T, 4], BF16, name="x_in", align_bytes=64)
+        pairs = keep.tile([P, 2 * T], U32, name="pairs", tag="pairs", align_bytes=64)
         x_codes = keep.tile([P, T], U32, name="x_codes", align_bytes=64)
         x_scales = keep.tile([P, T], U8, name="x_scales", align_bytes=64)
         g_codes = keep.tile([P, S], U32, name="g_codes", align_bytes=64)
         g_scales = keep.tile([P, S], U8, name="g_scales", align_bytes=64)
-        hs_codes = keep.tile([P, T], U32, name="hs_codes", align_bytes=64)
+        hs_codes = keep.tile([P, T], U32, name="hs_codes", tag="hs_codes", align_bytes=64)
         hs_scales = keep.tile([P, T], U8, name="hs_scales", align_bytes=64)
         windows = [keep.tile([P, T], F32, name=f"window{h}") for h in range(HALVES)]
         results = [keep.tile([P, T], F32, name=f"result{h}") for h in range(HALVES)]
 
         x_rows = xT.rearrange("(p j) t -> p j t", j=4)
 
-        def load_words(eng, tile, words, e0, e1):
-            eng.dma_start(
-                out=tile[:, e0:e1, :].bitcast(I32),
-                in_=words[e0:e1, 0].rearrange("e p b -> p e b").bitcast(I32),
-            )
+        def load_words(tile, words):
+            nc.sync.dma_start(out=tile.bitcast(I32), in_=words[:, 0].rearrange("e p b -> p e b").bitcast(I32))
 
-        def load_scales(eng, tile, scales, r):
+        def load_scales(eng, tile, scales, queues):
+            eng.memset(tile.rearrange("p e c -> p (e c)").bitcast(I32), 0)
             rows = scales[:, 0].rearrange("e (q r) c -> r q e c", r=4)
-            eng.dma_start(out=tile[r:P:32, :, :].bitcast(I32), in_=rows[r].bitcast(I32))
+            for r in range(4):
+                queues[r].dma_start(out=tile[r:P:32, :, :].bitcast(I32), in_=rows[r].bitcast(I32))
 
-        def zero_plane(eng, tile):
-            eng.memset(tile[:].rearrange("p e c -> p (e c)").bitcast(I32), 0)
-
-        def touch(words):
-            nc.gpsimd.memset(words.bitcast(I32), 0)
-
-        nc.sync.dma_start(out=x_a[:], in_=x_rows[:, :, :X_SPLIT])
-        load_words(nc.sync, w1, w1_words, SHARED, SHARED + 1)
         nc.sync.dma_start(offsets[:], offs)
-        zero_plane(nc.gpsimd, s1)
-        for r in range(4):
-            load_scales(nc.sync, s1, w1_scales, r)
-        touch(x_b[:, 0, 0:1])
-        nc.sync.dma_start(out=x_b[:], in_=x_rows[:, :, X_SPLIT:])
-        touch(w3[:, SHARED, 0:4])
-        load_words(nc.sync, w3, w3_words, SHARED, SHARED + 1)
-        zero_plane(nc.gpsimd, s3)
-        for r in range(4):
-            load_scales(nc.sync, s3, w3_scales, r)
-        touch(w1[:, 0, 0:4])
-        load_words(nc.sync, w1, w1_words, 0, E)
-        touch(w3[:, 0, 0:4])
-        load_words(nc.sync, w3, w3_words, 0, E)
-        zero_plane(nc.gpsimd, s2)
-        for r in range(4):
-            load_scales(nc.sync, s2, w2_scales, r)
-        touch(w2[:, 0, 0:4])
-        load_words(nc.sync, w2, w2_words, 0, E + 1)
-        touch(gates[:, 0, 0:1])
-        nc.sync.dma_start(out=gates[:], in_=gate.rearrange("(h p) s -> p h s", p=P))
+        nc.sync.dma_start(out=x_low[:], in_=x_rows[:, 0:2, :])
+        nc.sync.dma_start(out=x_high[0][:], in_=x_rows[:, 2:4, :X_SPLIT])
+        nc.sync.dma_start(out=x_high[1][:], in_=x_rows[:, 2:4, X_SPLIT:])
+        load_words(w1[:], w1_words)
+        load_scales(nc.gpsimd, s1[:], w1_scales, [nc.sync] * 4)
+        load_scales(nc.vector, s3[:], w3_scales, [nc.sync] * 2 + [nc.gpsimd] * 2)
+        nc.vector.memset(windows[0][:], 0.0)
         make_identity(nc, ident[:])
-        nc.vector.memset(warm[:], 0.0)
-        nc.scalar.activation(warm[:], warm[:], RELU)
-        for h in range(HALVES):
-            nc.vector.memset(windows[h][:], 0.0)
+        nc.scalar.activation(windows[1][:], windows[0][:], RELU)
 
-        def x_part(t0, t1):
-            return x_a[:, :, t0:t1] if t1 <= X_SPLIT else x_b[:, :, t0 - X_SPLIT : t1 - X_SPLIT]
-
-        def lay_shared(eng_copy, t0, t1):
-            eng_copy(out=x_in[:, t0:t1, :], in_=x_part(t0, t1).rearrange("p j t -> p t j"))
-
-        def quantize_shared(t0, t1):
-            nc.vector.quantize_mx(
-                out=x_codes[:, t0:t1].bitcast(FP8X4),
-                scales=x_scales[:, t0:t1],
-                in_=x_in[:, t0:t1, :].rearrange("p t j -> p (t j)"),
-            )
-
-        def cast_pairs(copy, u, t0, t1):
+        def cast_pairs(copy, u, t0, rows):
+            t1 = t0 + rows.shape[2]
             copy(
-                out=pairs[u][:, t0:t1].bitcast(BF16).rearrange("p (t d) -> p t d", d=2),
-                in_=x_part(t0, t1)[:, 2 * u : 2 * u + 2, :].rearrange("p d t -> p t d"),
+                out=pairs[:, u * T + t0 : u * T + t1].bitcast(BF16).rearrange("p (t d) -> p t d", d=2),
+                in_=rows.rearrange("p d t -> p t d"),
             )
 
-        def gather(j0, j1):
-            grouped = work.tile([P, j1 - j0, 2], U32, name="grouped", align_bytes=64)
-            for u in range(2):
-                nc.vector.tensor_copy(
-                    out=grouped[:, :, u], in_=pairs[u][:].indirect(offsets[:, j0 // 16 : j1 // 16])
-                )
-            nc.vector.quantize_mx(
-                out=g_codes[:, j0:j1].bitcast(FP8X4),
-                scales=g_scales[:, j0:j1],
-                in_=grouped[:].rearrange("p s u -> p (s u)").bitcast(BF16),
+        def weave(copy, dtype, planes, width, t0, t1, tag):
+            woven = keep.tile([P, 2 * (t1 - t0)], U32, name="woven", tag=tag, align_bytes=64)
+            copy(
+                out=woven[:].bitcast(dtype).rearrange("p (t u) -> p t u", u=2),
+                in_=planes.bitcast(dtype).rearrange("p (u t) -> p t u", t=width)[:, t0:t1, :],
+            )
+            return woven
+
+        def quantize(woven, codes, scales):
+            nc.vector.quantize_mx(out=codes.bitcast(FP8X4), scales=scales, in_=woven.bitcast(BF16))
+
+        def gather(picked, u, j0):
+            nc.vector.tensor_copy(
+                out=picked[:, u * 2 * C : (u + 1) * 2 * C],
+                in_=pairs[:, u * T : (u + 1) * T].indirect(offsets[:, j0 // 16 : (j0 + 2 * C) // 16]),
             )
 
-        def first_product(codes, scales, cols, words, planes, e, tag, bufs):
-            bank = psum.tile([P, H], F32, name="bank_" + tag, tag=tag, bufs=bufs)
+        def first_product(codes, scales, cols, words, planes, e):
+            bank = psum.tile([P, H], F32, name="bank", tag="sums", bufs=5)
             nc.tensor.matmul_mx(
                 out=bank[:],
                 lhsT=codes[:, cols].bitcast(FP8X4),
@@ -150,35 +111,28 @@ def tile_moe_shr_glu_relu_kernel(
             )
             return bank
 
-        def relu_side(e, codes, scales, cols):
-            bank = first_product(codes, scales, cols, w1, s1, e, "a", 2)
-            positive = work.tile([P, H], F32, name="positive", bufs=9)
+        def relu_side(e, codes, scales, cols, tag):
+            bank = first_product(codes, scales, cols, w1, s1, e)
+            positive = keep.tile([P, H], F32, name="positive", tag=tag, align_bytes=64)
             nc.scalar.activation(positive[:], bank[:], RELU)
             return positive
 
         def factor_side(e, codes, scales, cols, positive):
-            bank = first_product(codes, scales, cols, w3, s3, e, "b", 3)
+            bank = first_product(codes, scales, cols, w3, s3, e)
             hidden = work.tile([P, H], BF16, name="hidden", align_bytes=64)
             nc.vector.tensor_tensor(hidden[:], bank[:], positive[:], MULT)
             return hidden
 
-        def turn(group):
+        def turn(group, tag):
             n = len(group)
             bank = psum.tile([P, n, 2, P], F32, name="bank_t", tag="t")
             for i, hidden in enumerate(group):
                 words = hidden[:].bitcast(F32)
                 for u in range(2):
                     nc.tensor.transpose(bank[:, i, u, :], words[:, u::2], ident[:])
-            turned = work.tile([P, n, P, 2], F32, name="turned", align_bytes=64)
+            turned = keep.tile([P, n, P, 2], F32, name="turned", tag=tag, align_bytes=64)
             nc.scalar.copy(out=turned[:], in_=bank[:].rearrange("p i u r -> p i r u"))
-            return turned
-
-        def quantize_hidden(turned, codes, scales):
-            nc.vector.quantize_mx(
-                out=codes.bitcast(FP8X4),
-                scales=scales,
-                in_=turned[:].rearrange("p i r u -> p (i r u)").bitcast(BF16),
-            )
+            return turned[:].rearrange("p i r u -> p (i r u)")
 
         def layer2(e, h, bank, codes, scales):
             nc.tensor.matmul_mx(
@@ -191,107 +145,103 @@ def tile_moe_shr_glu_relu_kernel(
                 stop=True,
             )
 
-        def experts_out(e0, n, turned):
-            codes = work.tile([P, n, C], U32, name="h_codes", align_bytes=64)
-            scales = work.tile([P, n, C], U8, name="h_scales", align_bytes=64)
-            quantize_hidden(turned, codes[:].rearrange("p n c -> p (n c)"), scales[:].rearrange("p n c -> p (n c)"))
-            bank = psum.tile([P, HALVES, n * C], F32, name="bank_y", tag="y", bufs=1)
-            for i in range(n):
-                for h in range(HALVES):
-                    layer2(e0 + i, h, bank[:, h, i * C : (i + 1) * C], codes[:, i, :], scales[:, i, :])
-            y = work.tile([P, HALVES, n * C], F32, name="y")
-            nc.scalar.copy(out=y[:], in_=bank[:])
-            return y
-
-        def scatter(e0, n, h, y):
-            nc.vector.tensor_tensor(
-                windows[h][:].indirect(offsets[:, e0 * C // 16 : (e0 + n) * C // 16]),
-                y[:, h, :],
-                gates[:, h, e0 * C : (e0 + n) * C],
-                MULT,
-            )
-
         def cols(i, n=1):
             return slice(i * P, (i + n) * P)
 
-        chunks = T // P
-        groups = [(0, 2), (2, 2), (4, 1), (5, 2), (7, 2)]
-        hidden = {}
-        turned = {}
-        ys = {}
-        total = chunks + E
+        def routed_products(half, bank, e0, n):
+            for i in range(n):
+                layer2(e0 + i, half, bank[:, cols(i)], h_codes[:, cols(e0 + i)], h_scales[:, cols(e0 + i)])
 
-        positive = {}
+        def leave(bank, tag):
+            y = keep.tile([P, 2 * C], F32, name="y", tag=tag, align_bytes=64)
+            nc.scalar.copy(out=y[:], in_=bank)
+            return y
 
-        def where(c):
-            if c < chunks:
-                return SHARED, x_codes, x_scales, cols(c)
-            return c - chunks, g_codes, g_scales, cols(c - chunks)
+        def scatter(e0, half, y):
+            nc.vector.tensor_tensor(
+                windows[half][:].indirect(offsets[:, e0 * C // 16 : (e0 + 2) * C // 16]),
+                y[:],
+                gates[:, cols(e0, 2)],
+                MULT,
+            )
 
-        def a_step(c):
-            positive[c] = relu_side(*where(c))
+        def positive_shared(i):
+            return relu_side(SHARED, x_codes, x_scales, cols(i), f"positive_s{i}")
 
-        def b_step(c):
-            hidden[c] = factor_side(*where(c), positive[c])
+        def hidden_shared(i, positive):
+            return factor_side(SHARED, x_codes, x_scales, cols(i), positive)
 
-        def finish(g):
-            c, n = groups[g]
-            if c < chunks:
-                quantize_hidden(turned[g], hs_codes[:, cols(c, n)], hs_scales[:, cols(c, n)])
-            else:
-                ys[g] = experts_out(c - chunks, n, turned[g])
+        def hidden_routed(e):
+            positive = relu_side(e, g_codes, g_scales, cols(e), f"positive_r{e}")
+            return factor_side(e, g_codes, g_scales, cols(e), positive)
 
-        lay_shared(nc.vector.tensor_copy, 0, 128)
-        lay_shared(nc.vector.tensor_copy, 128, 256)
-        quantize_shared(0, 128)
-        quantize_shared(128, 256)
-        cast_pairs(nc.vector.tensor_copy, 0, 0, 256)
-        cast_pairs(nc.vector.tensor_copy, 1, 0, 256)
-        cast_pairs(nc.vector.tensor_copy, 0, 256, 640)
-        cast_pairs(nc.vector.tensor_copy, 1, 256, 640)
-        a_step(0)
-        a_step(1)
-        lay_shared(nc.vector.tensor_copy, 256, 640)
-        quantize_shared(256, 512)
-        quantize_shared(512, 640)
-        gather(0, 256)
-        gather(256, 512)
-        a_step(2)
-        a_step(3)
-        a_step(4)
-        b_step(0)
-        b_step(1)
-        a_step(5)
-        b_step(5)
-        a_step(6)
-        b_step(6)
-        turned[0] = turn([hidden[0], hidden[1]])
-        a_step(7)
-        b_step(7)
-        turned[3] = turn([hidden[5], hidden[6]])
-        a_step(8)
-        b_step(8)
-        finish(0)
-        finish(3)
-        turned[4] = turn([hidden[7], hidden[8]])
-        b_step(2)
-        finish(4)
-        b_step(3)
-        turned[1] = turn([hidden[2], hidden[3]])
-        b_step(4)
-        turned[2] = turn([hidden[4]])
-        finish(1)
-        finish(2)
-        tail = psum.tile([P, HALVES, P], F32, name="bank_tail", tag="a")
+        def weave_tokens(copy, dtype, i, n):
+            return weave(copy, dtype, pairs[:], T, i * P, (i + n) * P, f"tokens{i}")
+
+        def quantize_into(source, codes, scales, i, n):
+            quantize(source, codes[:, cols(i, n)], scales[:, cols(i, n)])
+
+        h_codes = keep.tile([P, S], U32, name="h_codes", align_bytes=64)
+        h_scales = keep.tile([P, S], U8, name="h_scales", align_bytes=64)
+        picked = [keep.tile([P, 4 * C], U32, name="picked", tag=f"picked{g}", align_bytes=64) for g in range(2)]
+        cast_pairs(nc.vector.tensor_copy, 0, 0, x_low[:])
+        w3 = keep.tile([P, E + 1, 2 * H], U8, name="w3", tag="x_low", align_bytes=64)
+        load_words(w3[:], w3_words)
+        cast_pairs(nc.scalar.copy, 1, 0, x_high[0][:])
+        cast_pairs(nc.scalar.copy, 1, X_SPLIT, x_high[1][:])
+        first_tokens = weave_tokens(nc.scalar.copy, U32, 0, 2)
+        for u in range(2):
+            for g in range(2):
+                gather(picked[g], u, g * 2 * C)
+        slots = [weave(nc.scalar.copy, U32, picked[g][:], 2 * C, 0, 2 * C, f"slots{g}") for g in range(2)]
+        quantize_into(first_tokens[:], x_codes, x_scales, 0, 2)
+        quantize_into(slots[0][:], g_codes, g_scales, 0, 2)
+        quantize_into(slots[1][:], g_codes, g_scales, 2, 2)
+        later_tokens = weave_tokens(nc.vector.tensor_copy, I32, 2, 3)
+        quantize_into(later_tokens[:, : 4 * P], x_codes, x_scales, 2, 2)
+        quantize_into(later_tokens[:, 4 * P :], x_codes, x_scales, 4, 1)
+        gates = keep.tile([P, S], F32, name="gates", tag="picked0", align_bytes=64)
+        nc.sync.dma_start(out=gates[:], in_=gate[0:P, :])
+        second = keep.tile([P, (E + 1) * 3 * N], U8, name="second", tag="tokens0", align_bytes=64)
+        s2 = second[:, : (E + 1) * N].rearrange("p (e c) -> p e c", c=N)
+        w2 = second[:, (E + 1) * N :].rearrange("p (e b) -> p e b", b=2 * N)
+        load_words(w2, w2_words)
+        load_scales(nc.gpsimd, s2, w2_scales, [nc.sync] * 4)
+
+        hs = [hidden_shared(i, positive_shared(i)) for i in range(2)]
+        h = [hidden_routed(e) for e in range(E)]
+        quantize_into(turn(h[0:2], "turned_r0"), h_codes, h_scales, 0, 2)
+        bank = psum.tile([P, 2 * C], F32, name="bank_y", tag="y", bufs=1)
+        routed_products(0, bank, 0, 2)
+        hs.append(hidden_shared(2, positive_shared(2)))
+        quantize_into(turn(h[2:4], "turned_r2"), h_codes, h_scales, 2, 2)
+        y_first = leave(bank[:], "y_first")
+        quantize_into(turn(hs[0:2], "turned_s0"), hs_codes, hs_scales, 0, 2)
+        scatter(0, 0, y_first)
+        bank = psum.tile([P, 2 * C], F32, name="bank_y", tag="y", bufs=1)
+        routed_products(0, bank, 2, 2)
+        hs.extend([hidden_shared(i, positive_shared(i)) for i in range(3, 5)])
+        scatter(2, 0, leave(bank[:], "positive_s3"))
+        upper = psum.tile([P, S], F32, name="bank_y", tag="y", bufs=1)
+        routed_products(1, upper, 0, E)
+        quantize_into(turn(hs[2:4], "turned_s2"), hs_codes, hs_scales, 2, 2)
+        quantize_into(turn(hs[4:5], "turned_s4"), hs_codes, hs_scales, 4, 1)
+        tail = psum.tile([P, HALVES, P], F32, name="bank_tail", tag="sums", bufs=5)
         bodies = []
-        for h in range(HALVES):
-            body = psum.tile([P, 512], F32, name="bank_body", tag="b", bufs=3)
-            layer2(SHARED, h, body[:], hs_codes[:, 0:512], hs_scales[:, 0:512])
-            layer2(SHARED, h, tail[:, h, :], hs_codes[:, 512:640], hs_scales[:, 512:640])
+        for half in range(HALVES):
+            body = psum.tile([P, 512], F32, name="bank_body", tag="sums", bufs=5)
+            layer2(SHARED, half, body[:], hs_codes[:, 0:512], hs_scales[:, 0:512])
+            layer2(SHARED, half, tail[:, half, :], hs_codes[:, 512:640], hs_scales[:, 512:640])
             bodies.append(body)
-        for h in range(HALVES):
-            scatter(0, 2, h, ys[3])
-            scatter(2, 2, h, ys[4])
-            for bank, t0, t1 in ((bodies[h][:], 0, 512), (tail[:, h, :], 512, 640)):
-                nc.vector.tensor_tensor(results[h][:, t0:t1], bank, windows[h][:, t0:t1], ADD)
-                nc.sync.dma_start(out=out[h * P : (h + 1) * P, t0:t1], in_=results[h][:, t0:t1])
+
+        def finish(half):
+            for source, t0, t1 in ((bodies[half][:], 0, 512), (tail[:, half, :], 512, 640)):
+                nc.vector.tensor_tensor(results[half][:, t0:t1], source, windows[half][:, t0:t1], ADD)
+                nc.sync.dma_start(out=out[half * P : (half + 1) * P, t0:t1], in_=results[half][:, t0:t1])
+
+        scatter(0, 1, leave(upper[:, cols(0, 2)], "turned_s2"))
+        finish(0)
+        y_last = keep.tile([P, 2 * C], F32, name="y_last", tag="hs_codes", align_bytes=64)
+        nc.scalar.copy(out=y_last[:], in_=upper[:, cols(2, 2)])
+        scatter(2, 1, y_last)
+        finish(1)

@@ -37,13 +37,16 @@ def tile_moe_shr_glu_relu_kernel(
 
         offsets = keep.tile([P, S // 16], U16, name="offsets")
         x_low = keep.tile([P, 2, T], F32, name="x_low", tag="x_low", align_bytes=64)
-        x_high = [keep.tile([P, 2, n], F32, name=f"x_high{n}") for n in (X_SPLIT, T - X_SPLIT)]
+        x_high = [
+            keep.tile([P, 2, n], F32, name="x_high", tag=f"x_high{i}", align_bytes=64)
+            for i, n in enumerate((X_SPLIT, T - X_SPLIT))
+        ]
         w1 = keep.tile([P, E + 1, 2 * H], U8, name="w1", align_bytes=64)
         s1 = keep.tile([P, E + 1, H], U8, name="s1", align_bytes=64)
         s3 = keep.tile([P, E + 1, H], U8, name="s3", align_bytes=64)
         ident = keep.tile([P, P], F32, name="ident")
         pairs = keep.tile([P, 2 * T], U32, name="pairs", tag="pairs", align_bytes=64)
-        x_codes = keep.tile([P, T], U32, name="x_codes", align_bytes=64)
+        x_codes = keep.tile([P, T], U32, name="x_codes", tag="x_codes", align_bytes=64)
         x_scales = keep.tile([P, T], U8, name="x_scales", align_bytes=64)
         g_codes = keep.tile([P, S], U32, name="g_codes", align_bytes=64)
         g_scales = keep.tile([P, S], U8, name="g_scales", align_bytes=64)
@@ -81,11 +84,11 @@ def tile_moe_shr_glu_relu_kernel(
                 in_=rows.rearrange("p d t -> p t d"),
             )
 
-        def weave(copy, dtype, planes, width, t0, t1, tag):
+        def weave(planes, width, t0, t1, tag):
             woven = keep.tile([P, 2 * (t1 - t0)], U32, name="woven", tag=tag, align_bytes=64)
-            copy(
-                out=woven[:].bitcast(dtype).rearrange("p (t u) -> p t u", u=2),
-                in_=planes.bitcast(dtype).rearrange("p (u t) -> p t u", t=width)[:, t0:t1, :],
+            nc.scalar.copy(
+                out=woven[:].rearrange("p (t u) -> p t u", u=2),
+                in_=planes.rearrange("p (u t) -> p t u", t=width)[:, t0:t1, :],
             )
             return woven
 
@@ -117,9 +120,9 @@ def tile_moe_shr_glu_relu_kernel(
             nc.scalar.activation(positive[:], bank[:], RELU)
             return positive
 
-        def factor_side(e, codes, scales, cols, positive):
+        def factor_side(e, codes, scales, cols, positive, tag):
             bank = first_product(codes, scales, cols, w3, s3, e)
-            hidden = work.tile([P, H], BF16, name="hidden", align_bytes=64)
+            hidden = keep.tile([P, H], BF16, name="hidden", tag=tag, align_bytes=64)
             nc.vector.tensor_tensor(hidden[:], bank[:], positive[:], MULT)
             return hidden
 
@@ -165,18 +168,24 @@ def tile_moe_shr_glu_relu_kernel(
                 MULT,
             )
 
-        def positive_shared(i):
-            return relu_side(SHARED, x_codes, x_scales, cols(i), f"positive_s{i}")
+        def hidden_run(chunks):
+            positive = {}
+            hidden = []
+            for n, (e, codes, scales, i) in enumerate(chunks):
+                for m in range(n, min(n + 2, len(chunks))):
+                    if m not in positive:
+                        ahead_e, ahead_codes, ahead_scales, ahead_i = chunks[m]
+                        positive[m] = relu_side(
+                            ahead_e, ahead_codes, ahead_scales, cols(ahead_i), f"positive_{ahead_e}_{ahead_i}"
+                        )
+                hidden.append(factor_side(e, codes, scales, cols(i), positive[n], f"hidden_{e}_{i}"))
+            return hidden
 
-        def hidden_shared(i, positive):
-            return factor_side(SHARED, x_codes, x_scales, cols(i), positive)
+        def shared_chunks(i0, i1):
+            return [(SHARED, x_codes, x_scales, i) for i in range(i0, i1)]
 
-        def hidden_routed(e):
-            positive = relu_side(e, g_codes, g_scales, cols(e), f"positive_r{e}")
-            return factor_side(e, g_codes, g_scales, cols(e), positive)
-
-        def weave_tokens(copy, dtype, i, n):
-            return weave(copy, dtype, pairs[:], T, i * P, (i + n) * P, f"tokens{i}")
+        def weave_tokens(i, n, tag):
+            return weave(pairs[:], T, i * P, (i + n) * P, tag)
 
         def quantize_into(source, codes, scales, i, n):
             quantize(source, codes[:, cols(i, n)], scales[:, cols(i, n)])
@@ -185,43 +194,43 @@ def tile_moe_shr_glu_relu_kernel(
         h_scales = keep.tile([P, S], U8, name="h_scales", align_bytes=64)
         picked = [keep.tile([P, 4 * C], U32, name="picked", tag=f"picked{g}", align_bytes=64) for g in range(2)]
         cast_pairs(nc.vector.tensor_copy, 0, 0, x_low[:])
+        cast_pairs(nc.scalar.copy, 1, 0, x_high[0][:])
         w3 = keep.tile([P, E + 1, 2 * H], U8, name="w3", tag="x_low", align_bytes=64)
         load_words(w3[:], w3_words)
-        cast_pairs(nc.scalar.copy, 1, 0, x_high[0][:])
         cast_pairs(nc.scalar.copy, 1, X_SPLIT, x_high[1][:])
-        first_tokens = weave_tokens(nc.scalar.copy, U32, 0, 2)
+
+        first_tokens = weave_tokens(0, 2, "tokens0")
         for u in range(2):
             for g in range(2):
                 gather(picked[g], u, g * 2 * C)
-        slots = [weave(nc.scalar.copy, U32, picked[g][:], 2 * C, 0, 2 * C, f"slots{g}") for g in range(2)]
+        slots = [weave(picked[g][:], 2 * C, 0, 2 * C, f"slots{g}") for g in range(2)]
         quantize_into(first_tokens[:], x_codes, x_scales, 0, 2)
         quantize_into(slots[0][:], g_codes, g_scales, 0, 2)
         quantize_into(slots[1][:], g_codes, g_scales, 2, 2)
-        later_tokens = weave_tokens(nc.vector.tensor_copy, I32, 2, 3)
+        later_tokens = weave_tokens(2, 3, "tokens2")
         quantize_into(later_tokens[:, : 4 * P], x_codes, x_scales, 2, 2)
         quantize_into(later_tokens[:, 4 * P :], x_codes, x_scales, 4, 1)
-        gates = keep.tile([P, S], F32, name="gates", tag="picked0", align_bytes=64)
-        nc.sync.dma_start(out=gates[:], in_=gate[0:P, :])
         second = keep.tile([P, (E + 1) * 3 * N], U8, name="second", tag="tokens0", align_bytes=64)
         s2 = second[:, : (E + 1) * N].rearrange("p (e c) -> p e c", c=N)
         w2 = second[:, (E + 1) * N :].rearrange("p (e b) -> p e b", b=2 * N)
         load_words(w2, w2_words)
         load_scales(nc.gpsimd, s2, w2_scales, [nc.sync] * 4)
+        gates = keep.tile([P, S], F32, name="gates", tag="picked0", align_bytes=64)
+        nc.sync.dma_start(out=gates[:], in_=gate[0:P, :])
 
-        hs = [hidden_shared(i, positive_shared(i)) for i in range(2)]
-        h = [hidden_routed(e) for e in range(E)]
+
+        first = hidden_run(shared_chunks(0, 2) + [(e, g_codes, g_scales, e) for e in range(E)])
+        hs, h = first[:2], first[2:]
         quantize_into(turn(h[0:2], "turned_r0"), h_codes, h_scales, 0, 2)
         bank = psum.tile([P, 2 * C], F32, name="bank_y", tag="y", bufs=1)
         routed_products(0, bank, 0, 2)
-        hs.append(hidden_shared(2, positive_shared(2)))
         quantize_into(turn(h[2:4], "turned_r2"), h_codes, h_scales, 2, 2)
-        y_first = leave(bank[:], "y_first")
-        quantize_into(turn(hs[0:2], "turned_s0"), hs_codes, hs_scales, 0, 2)
-        scatter(0, 0, y_first)
+        scatter(0, 0, leave(bank[:], "y_first"))
         bank = psum.tile([P, 2 * C], F32, name="bank_y", tag="y", bufs=1)
         routed_products(0, bank, 2, 2)
-        hs.extend([hidden_shared(i, positive_shared(i)) for i in range(3, 5)])
-        scatter(2, 0, leave(bank[:], "positive_s3"))
+        hs.extend(hidden_run(shared_chunks(2, 5)))
+        quantize_into(turn(hs[0:2], "turned_s0"), hs_codes, hs_scales, 0, 2)
+        scatter(2, 0, leave(bank[:], "x_codes"))
         upper = psum.tile([P, S], F32, name="bank_y", tag="y", bufs=1)
         routed_products(1, upper, 0, E)
         quantize_into(turn(hs[2:4], "turned_s2"), hs_codes, hs_scales, 2, 2)
@@ -239,7 +248,7 @@ def tile_moe_shr_glu_relu_kernel(
                 nc.vector.tensor_tensor(results[half][:, t0:t1], source, windows[half][:, t0:t1], ADD)
                 nc.sync.dma_start(out=out[half * P : (half + 1) * P, t0:t1], in_=results[half][:, t0:t1])
 
-        scatter(0, 1, leave(upper[:, cols(0, 2)], "turned_s2"))
+        scatter(0, 1, leave(upper[:, cols(0, 2)], "hidden_4_4"))
         finish(0)
         y_last = keep.tile([P, 2 * C], F32, name="y_last", tag="hs_codes", align_bytes=64)
         nc.scalar.copy(out=y_last[:], in_=upper[:, cols(2, 2)])

@@ -32,7 +32,6 @@ def tile_moe_shr_glu_relu_kernel(
     nc = tc.nc
     with ExitStack() as ctx:
         keep = ctx.enter_context(tc.tile_pool(name="keep", bufs=1))
-        work = ctx.enter_context(tc.tile_pool(name="work", bufs=6))
         psum = ctx.enter_context(tc.psum_pool(name="psum", bufs=2))
 
         offsets = keep.tile([P, S // 16], U16, name="offsets")
@@ -41,7 +40,7 @@ def tile_moe_shr_glu_relu_kernel(
             keep.tile([P, 2, n], F32, name="x_high", tag=f"x_high{i}", align_bytes=64)
             for i, n in enumerate((X_SPLIT, T - X_SPLIT))
         ]
-        w1 = keep.tile([P, E + 1, 2 * H], U8, name="w1", align_bytes=64)
+        w_shared = [keep.tile([P, 1, 2 * H], U8, name=f"w_shared{i}", align_bytes=64) for i in range(2)]
         s1 = keep.tile([P, E + 1, H], U8, name="s1", align_bytes=64)
         s3 = keep.tile([P, E + 1, H], U8, name="s3", align_bytes=64)
         ident = keep.tile([P, P], F32, name="ident")
@@ -60,19 +59,20 @@ def tile_moe_shr_glu_relu_kernel(
         def load_words(tile, words):
             nc.sync.dma_start(out=tile.bitcast(I32), in_=words[:, 0].rearrange("e p b -> p e b").bitcast(I32))
 
-        def load_scales(eng, tile, scales, queues):
+        def load_scales(eng, tile, scales):
             eng.memset(tile.rearrange("p e c -> p (e c)").bitcast(I32), 0)
             rows = scales[:, 0].rearrange("e (q r) c -> r q e c", r=4)
             for r in range(4):
-                queues[r].dma_start(out=tile[r:P:32, :, :].bitcast(I32), in_=rows[r].bitcast(I32))
+                nc.sync.dma_start(out=tile[r:P:32, :, :].bitcast(I32), in_=rows[r].bitcast(I32))
 
-        nc.sync.dma_start(offsets[:], offs)
         nc.sync.dma_start(out=x_low[:], in_=x_rows[:, 0:2, :])
+        nc.sync.dma_start(offsets[:], offs)
         nc.sync.dma_start(out=x_high[0][:], in_=x_rows[:, 2:4, :X_SPLIT])
         nc.sync.dma_start(out=x_high[1][:], in_=x_rows[:, 2:4, X_SPLIT:])
-        load_words(w1[:], w1_words)
-        load_scales(nc.gpsimd, s1[:], w1_scales, [nc.sync] * 4)
-        load_scales(nc.vector, s3[:], w3_scales, [nc.sync] * 2 + [nc.gpsimd] * 2)
+        load_words(w_shared[0][:], w1_words[SHARED:])
+        load_words(w_shared[1][:], w3_words[SHARED:])
+        load_scales(nc.gpsimd, s1[:], w1_scales)
+        load_scales(nc.vector, s3[:], w3_scales)
         nc.vector.memset(windows[0][:], 0.0)
         make_identity(nc, ident[:])
         nc.scalar.activation(windows[1][:], windows[0][:], RELU)
@@ -101,13 +101,14 @@ def tile_moe_shr_glu_relu_kernel(
                 in_=pairs[:, u * T : (u + 1) * T].indirect(offsets[:, j0 // 16 : (j0 + 2 * C) // 16]),
             )
 
-        def first_product(codes, scales, cols, words, planes, e):
+        def first_product(codes, scales, cols, side, planes, e):
+            words = w_shared[side][:, 0, :] if e == SHARED else w_routed[:, side * E + e, :]
             bank = psum.tile([P, H], F32, name="bank", tag="sums", bufs=5)
             nc.tensor.matmul_mx(
                 out=bank[:],
                 lhsT=codes[:, cols].bitcast(FP8X4),
                 lhsT_scale=scales[:, cols],
-                rhs=words[:, e, :].bitcast(FP4X4),
+                rhs=words.bitcast(FP4X4),
                 rhs_scale=planes[:, e, :],
                 start=True,
                 stop=True,
@@ -115,13 +116,13 @@ def tile_moe_shr_glu_relu_kernel(
             return bank
 
         def relu_side(e, codes, scales, cols, tag):
-            bank = first_product(codes, scales, cols, w1, s1, e)
+            bank = first_product(codes, scales, cols, 0, s1, e)
             positive = keep.tile([P, H], F32, name="positive", tag=tag, align_bytes=64)
             nc.scalar.activation(positive[:], bank[:], RELU)
             return positive
 
         def factor_side(e, codes, scales, cols, positive, tag):
-            bank = first_product(codes, scales, cols, w3, s3, e)
+            bank = first_product(codes, scales, cols, 1, s3, e)
             hidden = keep.tile([P, H], BF16, name="hidden", tag=tag, align_bytes=64)
             nc.vector.tensor_tensor(hidden[:], bank[:], positive[:], MULT)
             return hidden
@@ -195,8 +196,9 @@ def tile_moe_shr_glu_relu_kernel(
         picked = [keep.tile([P, 4 * C], U32, name="picked", tag=f"picked{g}", align_bytes=64) for g in range(2)]
         cast_pairs(nc.vector.tensor_copy, 0, 0, x_low[:])
         cast_pairs(nc.scalar.copy, 1, 0, x_high[0][:])
-        w3 = keep.tile([P, E + 1, 2 * H], U8, name="w3", tag="x_low", align_bytes=64)
-        load_words(w3[:], w3_words)
+        w_routed = keep.tile([P, 2 * E, 2 * H], U8, name="w_routed", tag="x_low", align_bytes=64)
+        load_words(w_routed[:, :E, :], w1_words[:E])
+        load_words(w_routed[:, E:, :], w3_words[:E])
         cast_pairs(nc.scalar.copy, 1, X_SPLIT, x_high[1][:])
 
         first_tokens = weave_tokens(0, 2, "tokens0")
@@ -214,7 +216,7 @@ def tile_moe_shr_glu_relu_kernel(
         s2 = second[:, : (E + 1) * N].rearrange("p (e c) -> p e c", c=N)
         w2 = second[:, (E + 1) * N :].rearrange("p (e b) -> p e b", b=2 * N)
         load_words(w2, w2_words)
-        load_scales(nc.gpsimd, s2, w2_scales, [nc.sync] * 4)
+        load_scales(nc.gpsimd, s2, w2_scales)
         gates = keep.tile([P, S], F32, name="gates", tag="picked0", align_bytes=64)
         nc.sync.dma_start(out=gates[:], in_=gate[0:P, :])
 

@@ -169,21 +169,22 @@ def tile_moe_shr_glu_relu_kernel(
                 MULT,
             )
 
-        def hidden_run(chunks):
-            positive = {}
-            hidden = []
-            for n, (e, codes, scales, i) in enumerate(chunks):
-                for m in range(n, min(n + 2, len(chunks))):
-                    if m not in positive:
-                        ahead_e, ahead_codes, ahead_scales, ahead_i = chunks[m]
-                        positive[m] = relu_side(
-                            ahead_e, ahead_codes, ahead_scales, cols(ahead_i), f"positive_{ahead_e}_{ahead_i}"
-                        )
-                hidden.append(factor_side(e, codes, scales, cols(i), positive[n], f"hidden_{e}_{i}"))
-            return hidden
+        def operands(e, i):
+            return (x_codes, x_scales, cols(i)) if e == SHARED else (g_codes, g_scales, cols(i))
 
-        def shared_chunks(i0, i1):
-            return [(SHARED, x_codes, x_scales, i) for i in range(i0, i1)]
+        positive = {}
+        hidden = {}
+
+        def relu_step(e, i):
+            positive[e, i] = relu_side(e, *operands(e, i), f"positive_{e}_{i}")
+
+        def product_step(e, i):
+            hidden[e, i] = factor_side(e, *operands(e, i), positive[e, i], f"hidden_{e}_{i}")
+
+        def run(chunks):
+            for done, ahead in zip(chunks, chunks[1:]):
+                relu_step(*ahead)
+                product_step(*done)
 
         def weave_tokens(i, n, tag):
             return weave(pairs[:], T, i * P, (i + n) * P, tag)
@@ -205,38 +206,47 @@ def tile_moe_shr_glu_relu_kernel(
         for u in range(2):
             for g in range(2):
                 gather(picked[g], u, g * 2 * C)
-        slots = [weave(picked[g][:], 2 * C, 0, 2 * C, f"slots{g}") for g in range(2)]
         quantize_into(first_tokens[:], x_codes, x_scales, 0, 2)
-        quantize_into(slots[0][:], g_codes, g_scales, 0, 2)
-        quantize_into(slots[1][:], g_codes, g_scales, 2, 2)
+        quantize_into(weave(picked[0][:], 2 * C, 0, 2 * C, "slots0")[:], g_codes, g_scales, 0, 2)
         later_tokens = weave_tokens(2, 3, "tokens2")
         quantize_into(later_tokens[:, : 4 * P], x_codes, x_scales, 2, 2)
         quantize_into(later_tokens[:, 4 * P :], x_codes, x_scales, 4, 1)
+        quantize_into(weave(picked[1][:], 2 * C, 0, 2 * C, "slots1")[:], g_codes, g_scales, 2, 2)
         second = keep.tile([P, (E + 1) * 3 * N], U8, name="second", tag="tokens0", align_bytes=64)
         s2 = second[:, : (E + 1) * N].rearrange("p (e c) -> p e c", c=N)
         w2 = second[:, (E + 1) * N :].rearrange("p (e b) -> p e b", b=2 * N)
         load_words(w2, w2_words)
         load_scales(nc.gpsimd, s2, w2_scales)
-        gates = keep.tile([P, S], F32, name="gates", tag="picked0", align_bytes=64)
+        gates = keep.tile([P, S], F32, name="gates", tag="slots1", align_bytes=64)
         nc.sync.dma_start(out=gates[:], in_=gate[0:P, :])
 
 
-        first = hidden_run(shared_chunks(0, 2) + [(e, g_codes, g_scales, e) for e in range(E)])
-        hs, h = first[:2], first[2:]
-        quantize_into(turn(h[0:2], "turned_r0"), h_codes, h_scales, 0, 2)
+        shared = [(SHARED, i) for i in range(T // P)]
+        routed = [(e, e) for e in range(E)]
+
+        def quantize_hidden(chunks, codes, scales):
+            e, i = chunks[0]
+            quantize_into(turn([hidden[c] for c in chunks], f"turned_{e}_{i}"), codes, scales, i, len(chunks))
+
+        relu_step(*shared[0])
+        run(shared[:3] + routed)
+        product_step(*routed[3])
+        quantize_hidden(routed[:2], h_codes, h_scales)
         bank = psum.tile([P, 2 * C], F32, name="bank_y", tag="y", bufs=1)
         routed_products(0, bank, 0, 2)
-        quantize_into(turn(h[2:4], "turned_r2"), h_codes, h_scales, 2, 2)
+        quantize_hidden(routed[2:], h_codes, h_scales)
         scatter(0, 0, leave(bank[:], "y_first"))
         bank = psum.tile([P, 2 * C], F32, name="bank_y", tag="y", bufs=1)
         routed_products(0, bank, 2, 2)
-        hs.extend(hidden_run(shared_chunks(2, 5)))
-        quantize_into(turn(hs[0:2], "turned_s0"), hs_codes, hs_scales, 0, 2)
+        relu_step(*shared[3])
+        run(shared[3:])
+        product_step(*shared[4])
+        quantize_hidden(shared[:2], hs_codes, hs_scales)
         scatter(2, 0, leave(bank[:], "x_codes"))
         upper = psum.tile([P, S], F32, name="bank_y", tag="y", bufs=1)
         routed_products(1, upper, 0, E)
-        quantize_into(turn(hs[2:4], "turned_s2"), hs_codes, hs_scales, 2, 2)
-        quantize_into(turn(hs[4:5], "turned_s4"), hs_codes, hs_scales, 4, 1)
+        quantize_hidden(shared[2:4], hs_codes, hs_scales)
+        quantize_hidden(shared[4:], hs_codes, hs_scales)
         tail = psum.tile([P, HALVES, P], F32, name="bank_tail", tag="sums", bufs=5)
         bodies = []
         for half in range(HALVES):

@@ -45,7 +45,7 @@ def tile_moe_shr_glu_relu_kernel(
         s3 = keep.tile([P, E + 1, H], U8, name="s3", align_bytes=64)
         ident = keep.tile([P, P], F32, name="ident")
         pairs = keep.tile([P, 2 * T], U32, name="pairs", tag="pairs", align_bytes=64)
-        x_codes = keep.tile([P, T], U32, name="x_codes", tag="x_codes", align_bytes=64)
+        x_codes = keep.tile([P, T], U32, name="x_codes", align_bytes=64)
         x_scales = keep.tile([P, T], U8, name="x_scales", align_bytes=64)
         g_codes = keep.tile([P, S], U32, name="g_codes", align_bytes=64)
         g_scales = keep.tile([P, S], U8, name="g_scales", align_bytes=64)
@@ -197,10 +197,15 @@ def tile_moe_shr_glu_relu_kernel(
         picked = [keep.tile([P, 4 * C], U32, name="picked", tag=f"picked{g}", align_bytes=64) for g in range(2)]
         cast_pairs(nc.vector.tensor_copy, 0, 0, x_low[:])
         cast_pairs(nc.scalar.copy, 1, 0, x_high[0][:])
-        w_routed = keep.tile([P, 2 * E, 2 * H], U8, name="w_routed", tag="x_low", align_bytes=64)
+        w_routed = keep.tile([P, 2 * E, 2 * H], U8, name="w_routed", tag="x_high0", align_bytes=64)
         load_words(w_routed[:, :E, :], w1_words[:E])
         load_words(w_routed[:, E:, :], w3_words[:E])
         cast_pairs(nc.scalar.copy, 1, X_SPLIT, x_high[1][:])
+        second = keep.tile([P, (E + 1) * 3 * N], U8, name="second", tag="x_high1", align_bytes=64)
+        s2 = second[:, : (E + 1) * N].rearrange("p (e c) -> p e c", c=N)
+        w2 = second[:, (E + 1) * N :].rearrange("p (e b) -> p e b", b=2 * N)
+        load_words(w2, w2_words)
+        load_scales(nc.gpsimd, s2, w2_scales)
 
         first_tokens = weave_tokens(0, 2, "tokens0")
         for u in range(2):
@@ -212,11 +217,6 @@ def tile_moe_shr_glu_relu_kernel(
         quantize_into(later_tokens[:, : 4 * P], x_codes, x_scales, 2, 2)
         quantize_into(later_tokens[:, 4 * P :], x_codes, x_scales, 4, 1)
         quantize_into(weave(picked[1][:], 2 * C, 0, 2 * C, "slots1")[:], g_codes, g_scales, 2, 2)
-        second = keep.tile([P, (E + 1) * 3 * N], U8, name="second", tag="tokens0", align_bytes=64)
-        s2 = second[:, : (E + 1) * N].rearrange("p (e c) -> p e c", c=N)
-        w2 = second[:, (E + 1) * N :].rearrange("p (e b) -> p e b", b=2 * N)
-        load_words(w2, w2_words)
-        load_scales(nc.gpsimd, s2, w2_scales)
         gates = keep.tile([P, S], F32, name="gates", tag="slots1", align_bytes=64)
         nc.sync.dma_start(out=gates[:], in_=gate[0:P, :])
 
@@ -224,45 +224,45 @@ def tile_moe_shr_glu_relu_kernel(
         shared = [(SHARED, i) for i in range(T // P)]
         routed = [(e, e) for e in range(E)]
 
-        def quantize_hidden(chunks, codes, scales):
-            e, i = chunks[0]
-            quantize_into(turn([hidden[c] for c in chunks], f"turned_{e}_{i}"), codes, scales, i, len(chunks))
+        def quantize_hidden(chunks, codes, scales, tag):
+            quantize_into(turn([hidden[c] for c in chunks], tag), codes, scales, chunks[0][1], len(chunks))
 
         relu_step(*shared[0])
         run(shared[:3] + routed)
         product_step(*routed[3])
-        quantize_hidden(routed[:2], h_codes, h_scales)
+        quantize_hidden(routed[:2], h_codes, h_scales, "turned_r0")
         bank = psum.tile([P, 2 * C], F32, name="bank_y", tag="y", bufs=1)
         routed_products(0, bank, 0, 2)
-        quantize_hidden(routed[2:], h_codes, h_scales)
+        quantize_hidden(routed[2:], h_codes, h_scales, "turned_r2")
         scatter(0, 0, leave(bank[:], "y_first"))
         bank = psum.tile([P, 2 * C], F32, name="bank_y", tag="y", bufs=1)
         routed_products(0, bank, 2, 2)
         relu_step(*shared[3])
         run(shared[3:])
         product_step(*shared[4])
-        quantize_hidden(shared[:2], hs_codes, hs_scales)
-        scatter(2, 0, leave(bank[:], "x_codes"))
+        quantize_hidden(shared[:2], hs_codes, hs_scales, "positive_4_3")
+        scatter(2, 0, leave(bank[:], "positive_4_4"))
         upper = psum.tile([P, S], F32, name="bank_y", tag="y", bufs=1)
         routed_products(1, upper, 0, E)
-        quantize_hidden(shared[2:4], hs_codes, hs_scales)
-        quantize_hidden(shared[4:], hs_codes, hs_scales)
-        tail = psum.tile([P, HALVES, P], F32, name="bank_tail", tag="sums", bufs=5)
-        bodies = []
+        quantize_hidden(shared[2:4], hs_codes, hs_scales, "turned_s2")
+        quantize_hidden(shared[4:], hs_codes, hs_scales, "turned_s4")
+        bodies, tails = [], []
         for half in range(HALVES):
-            body = psum.tile([P, 512], F32, name="bank_body", tag="sums", bufs=5)
-            layer2(SHARED, half, body[:], hs_codes[:, 0:512], hs_scales[:, 0:512])
-            layer2(SHARED, half, tail[:, half, :], hs_codes[:, 512:640], hs_scales[:, 512:640])
-            bodies.append(body)
+            bodies.append(psum.tile([P, 4 * P], F32, name="bank_body", tag="sums", bufs=5))
+            tails.append(psum.tile([P, P], F32, name="bank_tail", tag="sums", bufs=5))
+            layer2(SHARED, half, bodies[half][:], hs_codes[:, cols(0, 4)], hs_scales[:, cols(0, 4)])
+            layer2(SHARED, half, tails[half][:], hs_codes[:, cols(4)], hs_scales[:, cols(4)])
 
-        def finish(half):
-            for source, t0, t1 in ((bodies[half][:], 0, 512), (tail[:, half, :], 512, 640)):
-                nc.vector.tensor_tensor(results[half][:, t0:t1], source, windows[half][:, t0:t1], ADD)
-                nc.sync.dma_start(out=out[half * P : (half + 1) * P, t0:t1], in_=results[half][:, t0:t1])
+        def finish(engine, half, piece, shared_sums):
+            engine.tensor_tensor(results[half][:, piece], shared_sums, windows[half][:, piece], ADD)
+            nc.sync.dma_start(out=out[half * P : (half + 1) * P, piece], in_=results[half][:, piece])
 
         scatter(0, 1, leave(upper[:, cols(0, 2)], "hidden_4_4"))
-        finish(0)
-        y_last = keep.tile([P, 2 * C], F32, name="y_last", tag="hs_codes", align_bytes=64)
-        nc.scalar.copy(out=y_last[:], in_=upper[:, cols(2, 2)])
-        scatter(2, 1, y_last)
-        finish(1)
+        finish(nc.vector, 0, cols(0, 4), bodies[0][:])
+        finish(nc.vector, 0, cols(4), tails[0][:])
+        scatter(2, 1, leave(upper[:, cols(2, 2)], "hs_codes"))
+        last_tail = keep.tile([P, P], F32, name="last_tail")
+        nc.scalar.copy(out=last_tail[:], in_=tails[1][:])
+        finish(nc.gpsimd, 1, cols(4), last_tail[:])
+        for piece in (cols(0, 2), cols(2, 2)):
+            finish(nc.vector, 1, piece, bodies[1][:, piece])

@@ -20,6 +20,7 @@ U8 = mybir.dt.uint8
 FP8X4 = mybir.dt.float8_e4m3fn_x4
 FP4X4 = mybir.dt.float4_e2m1fn_x4
 RELU = mybir.ActivationFunctionType.Relu
+COPY = mybir.ActivationFunctionType.Copy
 MULT = mybir.AluOpType.mult
 ADD = mybir.AluOpType.add
 
@@ -52,7 +53,6 @@ def tile_moe_shr_glu_relu_kernel(
         hs_codes = keep.tile([P, T], U32, name="hs_codes", tag="hs_codes", align_bytes=64)
         hs_scales = keep.tile([P, T], U8, name="hs_scales", align_bytes=64)
         windows = [keep.tile([P, T], F32, name=f"window{h}") for h in range(HALVES)]
-        results = [keep.tile([P, T], F32, name=f"result{h}") for h in range(HALVES)]
 
         x_rows = xT.rearrange("(p j) t -> p j t", j=4)
 
@@ -235,34 +235,60 @@ def tile_moe_shr_glu_relu_kernel(
         routed_products(0, bank, 0, 2)
         quantize_hidden(routed[2:], h_codes, h_scales, "turned_r2")
         scatter(0, 0, leave(bank[:], "y_first"))
-        bank = psum.tile([P, 2 * C], F32, name="bank_y", tag="y", bufs=1)
-        routed_products(0, bank, 2, 2)
+        third = psum.tile([P, 2 * C], F32, name="bank_y", tag="y", bufs=1)
+        routed_products(0, third, 2, 2)
         relu_step(*shared[3])
         run(shared[3:])
         product_step(*shared[4])
+        second_bank = psum.tile([P, 2 * C], F32, name="bank_second", tag="sums", bufs=5)
+        routed_products(1, second_bank, 0, 2)
+        slot_gates = keep.tile([P, 2], F32, name="slot_gates", tag="positive_0_0", align_bytes=64)
+        with nc.allow_non_contiguous_dma(reason="one gate value a partition"):
+            nc.sync.dma_start(out=slot_gates[:], in_=gate[0, 2 * C :].rearrange("(j p) -> p j", p=P))
+        slot_major = psum.tile([P, 2, P], F32, name="bank_slots", tag="sums", bufs=5)
+        for j in range(2):
+            nc.tensor.matmul_mx(
+                out=slot_major[:, j, :],
+                lhsT=h_codes[:, cols(2 + j)].bitcast(FP8X4),
+                lhsT_scale=h_scales[:, cols(2 + j)],
+                rhs=w2[:, 2 + j, 2 * P :].bitcast(FP4X4),
+                rhs_scale=s2[:, 2 + j, P:],
+                start=True,
+                stop=True,
+            )
         quantize_hidden(shared[:2], hs_codes, hs_scales, "positive_4_3")
-        scatter(2, 0, leave(bank[:], "positive_4_4"))
-        upper = psum.tile([P, S], F32, name="bank_y", tag="y", bufs=1)
-        routed_products(1, upper, 0, E)
+        scatter(0, 1, leave(second_bank[:], "positive_4_4"))
         quantize_hidden(shared[2:4], hs_codes, hs_scales, "turned_s2")
+        by_slot = keep.tile([P, 2, P], F32, name="by_slot")
+        for j in range(2):
+            nc.scalar.activation(by_slot[:, j, :], slot_major[:, j, :], COPY, scale=slot_gates[:, j : j + 1])
+        back = psum.tile([P, 2, P], F32, name="bank_back", tag="sums", bufs=5)
+        for j in range(2):
+            nc.tensor.transpose(back[:, j, :], by_slot[:, j, :], ident[:])
         quantize_hidden(shared[4:], hs_codes, hs_scales, "turned_s4")
-        bodies, tails = [], []
+        scatter(2, 0, leave(third[:], "hidden_4_4"))
+        y_last = leave(back[:].rearrange("p j s -> p (j s)"), "turned_s2")
+        bodies = []
         for half in range(HALVES):
             bodies.append(psum.tile([P, 4 * P], F32, name="bank_body", tag="sums", bufs=5))
-            tails.append(psum.tile([P, P], F32, name="bank_tail", tag="sums", bufs=5))
             layer2(SHARED, half, bodies[half][:], hs_codes[:, cols(0, 4)], hs_scales[:, cols(0, 4)])
-            layer2(SHARED, half, tails[half][:], hs_codes[:, cols(4)], hs_scales[:, cols(4)])
+        tails = psum.tile([P, HALVES, P], F32, name="bank_tails", tag="sums", bufs=5)
+        for half in range(HALVES):
+            layer2(SHARED, half, tails[:, half, :], hs_codes[:, cols(4)], hs_scales[:, cols(4)])
 
         def finish(engine, half, piece, shared_sums):
             engine.tensor_tensor(results[half][:, piece], shared_sums, windows[half][:, piece], ADD)
             nc.sync.dma_start(out=out[half * P : (half + 1) * P, piece], in_=results[half][:, piece])
 
-        scatter(0, 1, leave(upper[:, cols(0, 2)], "hidden_4_4"))
-        finish(nc.vector, 0, cols(0, 4), bodies[0][:])
-        finish(nc.vector, 0, cols(4), tails[0][:])
-        scatter(2, 1, leave(upper[:, cols(2, 2)], "hs_codes"))
-        last_tail = keep.tile([P, P], F32, name="last_tail")
-        nc.scalar.copy(out=last_tail[:], in_=tails[1][:])
-        finish(nc.gpsimd, 1, cols(4), last_tail[:])
+        nc.vector.tensor_copy(windows[1][:].indirect(offsets[:, 2 * C // 16 :]), y_last[:])
+        results = [keep.tile([P, T], F32, name="result_low")]
+        body_sums = keep.tile([P, 4 * P], F32, name="body_sums", tag="body_sums")
+        nc.scalar.copy(out=body_sums[:], in_=bodies[0][:])
+        tail_sums = keep.tile([P, HALVES, P], F32, name="tail_sums")
+        nc.scalar.copy(out=tail_sums[:], in_=tails[:])
+        finish(nc.gpsimd, 0, cols(0, 4), body_sums[:])
+        results.append(keep.tile([P, T], F32, name="result_high", tag="body_sums"))
+        for half in range(HALVES):
+            finish(nc.gpsimd, half, cols(4), tail_sums[:, half, :])
         for piece in (cols(0, 2), cols(2, 2)):
             finish(nc.vector, 1, piece, bodies[1][:, piece])

@@ -115,16 +115,24 @@ def tile_moe_shr_glu_relu_kernel(
             )
             return bank
 
+        def by_pair(ap, pattern):
+            return ap.rearrange(pattern, u=2, d=2)
+
         def relu_side(e, codes, scales, cols, tag):
             bank = first_product(codes, scales, cols, 0, s1, e)
             positive = keep.tile([P, H], F32, name="positive", tag=tag, align_bytes=64)
-            nc.scalar.activation(positive[:], bank[:], RELU)
+            nc.scalar.activation(by_pair(positive[:], "p (u r d) -> p u r d"), by_pair(bank[:], "p (r u d) -> p u r d"), RELU)
             return positive
 
         def factor_side(e, codes, scales, cols, positive, tag):
             bank = first_product(codes, scales, cols, 1, s3, e)
             hidden = keep.tile([P, H], BF16, name="hidden", tag=tag, align_bytes=64)
-            nc.vector.tensor_tensor(hidden[:], bank[:], positive[:], MULT)
+            nc.vector.tensor_tensor(
+                by_pair(hidden[:], "p (u r d) -> p u r d"),
+                by_pair(bank[:], "p (r u d) -> p u r d"),
+                by_pair(positive[:], "p (u r d) -> p u r d"),
+                MULT,
+            )
             return hidden
 
         def turn(group, tag):
@@ -133,7 +141,7 @@ def tile_moe_shr_glu_relu_kernel(
             for i, hidden in enumerate(group):
                 words = hidden[:].bitcast(F32)
                 for u in range(2):
-                    nc.tensor.transpose(bank[:, i, u, :], words[:, u::2], ident[:])
+                    nc.tensor.transpose(bank[:, i, u, :], words[:, u * P : (u + 1) * P], ident[:])
             turned = keep.tile([P, n, P, 2], F32, name="turned", tag=tag, align_bytes=64)
             nc.scalar.copy(out=turned[:], in_=bank[:].rearrange("p i u r -> p i r u"))
             return turned[:].rearrange("p i r u -> p (i r u)")

@@ -284,9 +284,9 @@ def tile_moe_shr_glu_relu_kernel(
         for half in range(HALVES):
             layer2(SHARED, half, tails[:, half, :], hs_codes[:, cols(4)], hs_scales[:, cols(4)])
 
-        def finish(engine, half, piece, shared_sums):
+        def finish(engine, half, piece, shared_sums, queue=nc.sync):
             engine.tensor_tensor(results[half][:, piece], shared_sums, windows[half][:, piece], ADD)
-            nc.sync.dma_start(out=out[half * P : (half + 1) * P, piece], in_=results[half][:, piece])
+            queue.dma_start(out=out[half * P : (half + 1) * P, piece], in_=results[half][:, piece])
 
         nc.vector.tensor_copy(windows[1][:].indirect(offsets[:, 2 * C // 16 :]), y_last[:])
         results = [keep.tile([P, T], F32, name="result_low")]
@@ -298,5 +298,5 @@ def tile_moe_shr_glu_relu_kernel(
         results.append(keep.tile([P, T], F32, name="result_high", tag="body_sums"))
         for half in range(HALVES):
             finish(nc.gpsimd, half, cols(4), tail_sums[:, half, :])
-        for piece in (cols(0, 2), cols(2, 2)):
-            finish(nc.vector, 1, piece, bodies[1][:, piece])
+        for piece in (slice(0, 320), slice(320, 512)):
+            finish(nc.vector, 1, piece, bodies[1][:, piece], nc.scalar)

@@ -9,7 +9,6 @@ K, T, E, C, H, N = 512, 640, 4, 128, 512, 256
 S = E * C
 SHARED = E
 P = 128
-HALVES = N // P
 
 F32 = mybir.dt.float32
 BF16 = mybir.dt.bfloat16
@@ -33,37 +32,146 @@ def tile_moe_shr_glu_relu_kernel(
     nc = tc.nc
     with ExitStack() as ctx:
         keep = ctx.enter_context(tc.tile_pool(name="keep", bufs=1))
-        psum = ctx.enter_context(tc.psum_pool(name="psum", bufs=2))
+        psum = ctx.enter_context(tc.psum_pool(name="psum", bufs=1))
+
+        def sb(shape, dtype, name, tag=None):
+            return keep.tile(shape, dtype, name=name, tag=tag or name, align_bytes=64)
+
+        def bank(number, shape):
+            return psum.tile(shape, F32, name="bank", tag=f"bank{number}")
+
+        def cols(i, n=1):
+            return slice(i * P, (i + n) * P)
 
         offsets = keep.tile([P, S // 16], U16, name="offsets")
-        x_low = keep.tile([P, 2, T], F32, name="x_low", tag="x_low", align_bytes=64)
-        x_high = [
-            keep.tile([P, 2, n], F32, name="x_high", tag=f"x_high{i}", align_bytes=64)
-            for i, n in enumerate((X_SPLIT, T - X_SPLIT))
-        ]
-        w_shared = [keep.tile([P, 1, 2 * H], U8, name=f"w_shared{i}", align_bytes=64) for i in range(2)]
-        s1 = keep.tile([P, E + 1, H], U8, name="s1", align_bytes=64)
-        s3 = keep.tile([P, E + 1, H], U8, name="s3", align_bytes=64)
-        ident = keep.tile([P, P], F32, name="ident")
-        pairs = keep.tile([P, 2 * T], U32, name="pairs", tag="pairs", align_bytes=64)
-        x_codes = keep.tile([P, T], U32, name="x_codes", align_bytes=64)
-        x_scales = keep.tile([P, T], U8, name="x_scales", align_bytes=64)
-        g_codes = keep.tile([P, S], U32, name="g_codes", align_bytes=64)
-        g_scales = keep.tile([P, S], U8, name="g_scales", align_bytes=64)
-        hs_codes = keep.tile([P, T], U32, name="hs_codes", tag="hs_codes", align_bytes=64)
-        hs_scales = keep.tile([P, T], U8, name="hs_scales", align_bytes=64)
-        windows = [keep.tile([P, T], F32, name=f"window{h}") for h in range(HALVES)]
+        x_low = sb([P, 2, T], F32, "x_low")
+        x_high = [sb([P, 2, n], F32, f"x_high{i}") for i, n in enumerate((X_SPLIT, T - X_SPLIT))]
+        w_shared = [sb([P, 1, 2 * H], U8, f"w_shared{i}") for i in range(2)]
+        s1 = sb([P, E + 1, H], U8, "s1")
+        s3 = sb([P, E + 1, H], U8, "s3")
+        ident = sb([P, P], F32, "ident")
+        pairs = sb([P, 2 * T], U32, "pairs")
+        x_codes, x_scales = sb([P, T], U32, "x_codes"), sb([P, T], U8, "x_scales")
+        g_codes, g_scales = sb([P, S], U32, "g_codes"), sb([P, S], U8, "g_scales")
+        hs_codes, hs_scales = sb([P, T], U32, "hs_codes"), sb([P, T], U8, "hs_scales")
+        h_codes, h_scales = sb([P, S], U32, "h_codes"), sb([P, S], U8, "h_scales")
+        picked = [sb([P, 4 * C], U32, f"picked{g}") for g in range(2)]
+        windows = [sb([P, T], F32, f"window{half}") for half in range(2)]
+        results = [sb([P, T], F32, f"result{half}") for half in range(2)]
 
         x_rows = xT.rearrange("(p j) t -> p j t", j=4)
 
         def load_words(tile, words):
             nc.sync.dma_start(out=tile.bitcast(I32), in_=words[:, 0].rearrange("e p b -> p e b").bitcast(I32))
 
-        def load_scales(eng, tile, scales):
-            eng.memset(tile.rearrange("p e c -> p (e c)").bitcast(I32), 0)
+        def load_scales(engine, tile, scales):
+            engine.memset(tile.rearrange("p e c -> p (e c)").bitcast(I32), 0)
             rows = scales[:, 0].rearrange("e (q r) c -> r q e c", r=4)
             for r in range(4):
                 nc.sync.dma_start(out=tile[r:P:32, :, :].bitcast(I32), in_=rows[r].bitcast(I32))
+
+        def cast_pairs(copy, u, t0, rows):
+            t1 = t0 + rows.shape[2]
+            copy(
+                out=pairs[:, u * T + t0 : u * T + t1].bitcast(BF16).rearrange("p (t d) -> p t d", d=2),
+                in_=rows.rearrange("p d t -> p t d"),
+            )
+
+        def weave(planes, width, t0, t1, name):
+            woven = sb([P, 2 * (t1 - t0)], U32, name)
+            nc.scalar.copy(
+                out=woven[:].rearrange("p (t u) -> p t u", u=2),
+                in_=planes.rearrange("p (u t) -> p t u", t=width)[:, t0:t1, :],
+            )
+            return woven
+
+        def quantize(words, codes, scales, i, n):
+            nc.vector.quantize_mx(out=codes[:, cols(i, n)].bitcast(FP8X4), scales=scales[:, cols(i, n)], in_=words.bitcast(BF16))
+
+        def listed(j0, n):
+            return offsets[:, j0 // 16 : (j0 + n) // 16]
+
+        def gather(g, u):
+            nc.vector.tensor_copy(
+                out=picked[g][:, u * 2 * C : (u + 1) * 2 * C],
+                in_=pairs[:, u * T : (u + 1) * T].indirect(listed(g * 2 * C, 2 * C)),
+            )
+
+        def product(sums, lhsT, lhsT_scale, rhs, rhs_scale):
+            nc.tensor.matmul_mx(out=sums, lhsT=lhsT, lhsT_scale=lhsT_scale, rhs=rhs, rhs_scale=rhs_scale, start=True, stop=True)
+
+        def first_layer(chunk, side, number):
+            e, i = chunk
+            codes, scales = (x_codes, x_scales) if e == SHARED else (g_codes, g_scales)
+            words = w_shared[side][:, 0, :] if e == SHARED else w_routed[:, side * E + e, :]
+            sums = bank(number, [P, H])
+            product(sums[:], codes[:, cols(i)].bitcast(FP8X4), scales[:, cols(i)], words.bitcast(FP4X4), (s1, s3)[side][:, e, :])
+            return sums
+
+        def in_pairs(ap, pattern):
+            return ap.rearrange(pattern, u=2, d=2)
+
+        positive = {}
+        hidden = {}
+
+        def relu_side(chunk, number):
+            sums = first_layer(chunk, 0, number)
+            positive[chunk] = sb([P, H], F32, "positive_%d_%d" % chunk)
+            nc.scalar.activation(in_pairs(positive[chunk][:], "p (u r d) -> p u r d"), in_pairs(sums[:], "p (r u d) -> p u r d"), RELU)
+
+        def factor_side(chunk, number):
+            sums = first_layer(chunk, 1, number)
+            hidden[chunk] = sb([P, H], BF16, "hidden_%d_%d" % chunk)
+            nc.vector.tensor_tensor(
+                in_pairs(hidden[chunk][:], "p (u r d) -> p u r d"),
+                in_pairs(sums[:], "p (r u d) -> p u r d"),
+                in_pairs(positive[chunk][:], "p (u r d) -> p u r d"),
+                MULT,
+            )
+
+        def turn_and_quantize(chunks, number):
+            e, i = chunks[0]
+            n = len(chunks)
+            turned_sums = bank(number, [P, n, 2, P])
+            for j, chunk in enumerate(chunks):
+                words = hidden[chunk][:].bitcast(F32)
+                for u in range(2):
+                    nc.tensor.transpose(turned_sums[:, j, u, :], words[:, cols(u)], ident[:])
+            turned = sb([P, n, P, 2], F32, "turned_%d_%d" % chunks[0])
+            nc.scalar.copy(out=turned[:], in_=turned_sums[:].rearrange("p i u r -> p i r u"))
+            codes, scales = (hs_codes, hs_scales) if e == SHARED else (h_codes, h_scales)
+            quantize(turned[:].rearrange("p i r u -> p (i r u)"), codes, scales, i, n)
+
+        def second_layer(e, half, sums, codes, scales):
+            product(sums, w2[:, e, 2 * P * half : 2 * P * (half + 1)].bitcast(FP4X4), s2[:, e, cols(half)], codes.bitcast(FP8X4), scales)
+
+        def routed_sums(e0, half, number):
+            sums = bank(number, [P, 2 * C])
+            for j in range(2):
+                second_layer(e0 + j, half, sums[:, cols(j)], h_codes[:, cols(e0 + j)], h_scales[:, cols(e0 + j)])
+            return sums
+
+        def leave_low(e0, number, tag=None):
+            sums = routed_sums(e0, 0, number)
+            y = sb([P, 2 * C], F32, f"y_low{e0}", tag)
+            nc.scalar.copy(out=y[:], in_=sums[:])
+            return y
+
+        def leave_high(e0, number):
+            sums = routed_sums(e0, 1, number)
+            y = sb([P, 2 * C], F32, f"y_high{e0}")
+            nc.vector.tensor_tensor(y[:], sums[:], gates[:, cols(e0, 2)], MULT)
+            return y
+
+        def scatter_low(e0, y):
+            nc.vector.tensor_tensor(windows[0][:].indirect(listed(e0 * C, 2 * C)), y[:], gates[:, cols(e0, 2)], MULT)
+
+        def scatter_high(e0, y):
+            nc.scalar.activation(windows[1][:].indirect(listed(e0 * C, 2 * C)), y[:], COPY)
+
+        def finish(half, piece, shared_sums, queue):
+            nc.vector.tensor_tensor(results[half][:, piece], shared_sums, windows[half][:, piece], ADD)
+            queue.dma_start(out=out[cols(half), piece], in_=results[half][:, piece])
 
         nc.sync.dma_start(out=x_low[:], in_=x_rows[:, 0:2, :])
         nc.sync.dma_start(offsets[:], offs)
@@ -77,226 +185,73 @@ def tile_moe_shr_glu_relu_kernel(
         make_identity(nc, ident[:])
         nc.scalar.activation(windows[1][:], windows[0][:], RELU)
 
-        def cast_pairs(copy, u, t0, rows):
-            t1 = t0 + rows.shape[2]
-            copy(
-                out=pairs[:, u * T + t0 : u * T + t1].bitcast(BF16).rearrange("p (t d) -> p t d", d=2),
-                in_=rows.rearrange("p d t -> p t d"),
-            )
-
-        def weave(planes, width, t0, t1, tag):
-            woven = keep.tile([P, 2 * (t1 - t0)], U32, name="woven", tag=tag, align_bytes=64)
-            nc.scalar.copy(
-                out=woven[:].rearrange("p (t u) -> p t u", u=2),
-                in_=planes.rearrange("p (u t) -> p t u", t=width)[:, t0:t1, :],
-            )
-            return woven
-
-        def quantize(woven, codes, scales):
-            nc.vector.quantize_mx(out=codes.bitcast(FP8X4), scales=scales, in_=woven.bitcast(BF16))
-
-        def gather(picked, u, j0):
-            nc.vector.tensor_copy(
-                out=picked[:, u * 2 * C : (u + 1) * 2 * C],
-                in_=pairs[:, u * T : (u + 1) * T].indirect(offsets[:, j0 // 16 : (j0 + 2 * C) // 16]),
-            )
-
-        def first_product(codes, scales, cols, side, planes, e):
-            words = w_shared[side][:, 0, :] if e == SHARED else w_routed[:, side * E + e, :]
-            bank = psum.tile([P, H], F32, name="bank", tag="sums", bufs=5)
-            nc.tensor.matmul_mx(
-                out=bank[:],
-                lhsT=codes[:, cols].bitcast(FP8X4),
-                lhsT_scale=scales[:, cols],
-                rhs=words.bitcast(FP4X4),
-                rhs_scale=planes[:, e, :],
-                start=True,
-                stop=True,
-            )
-            return bank
-
-        def by_pair(ap, pattern):
-            return ap.rearrange(pattern, u=2, d=2)
-
-        def relu_side(e, codes, scales, cols, tag):
-            bank = first_product(codes, scales, cols, 0, s1, e)
-            positive = keep.tile([P, H], F32, name="positive", tag=tag, align_bytes=64)
-            nc.scalar.activation(by_pair(positive[:], "p (u r d) -> p u r d"), by_pair(bank[:], "p (r u d) -> p u r d"), RELU)
-            return positive
-
-        def factor_side(e, codes, scales, cols, positive, tag):
-            bank = first_product(codes, scales, cols, 1, s3, e)
-            hidden = keep.tile([P, H], BF16, name="hidden", tag=tag, align_bytes=64)
-            nc.vector.tensor_tensor(
-                by_pair(hidden[:], "p (u r d) -> p u r d"),
-                by_pair(bank[:], "p (r u d) -> p u r d"),
-                by_pair(positive[:], "p (u r d) -> p u r d"),
-                MULT,
-            )
-            return hidden
-
-        def turn(group, tag):
-            n = len(group)
-            bank = psum.tile([P, n, 2, P], F32, name="bank_t", tag="t")
-            for i, hidden in enumerate(group):
-                words = hidden[:].bitcast(F32)
-                for u in range(2):
-                    nc.tensor.transpose(bank[:, i, u, :], words[:, u * P : (u + 1) * P], ident[:])
-            turned = keep.tile([P, n, P, 2], F32, name="turned", tag=tag, align_bytes=64)
-            nc.scalar.copy(out=turned[:], in_=bank[:].rearrange("p i u r -> p i r u"))
-            return turned[:].rearrange("p i r u -> p (i r u)")
-
-        def layer2(e, h, bank, codes, scales):
-            nc.tensor.matmul_mx(
-                out=bank,
-                lhsT=w2[:, e, 2 * P * h : 2 * P * (h + 1)].bitcast(FP4X4),
-                lhsT_scale=s2[:, e, P * h : P * (h + 1)],
-                rhs=codes.bitcast(FP8X4),
-                rhs_scale=scales,
-                start=True,
-                stop=True,
-            )
-
-        def cols(i, n=1):
-            return slice(i * P, (i + n) * P)
-
-        def routed_products(half, bank, e0, n):
-            for i in range(n):
-                layer2(e0 + i, half, bank[:, cols(i)], h_codes[:, cols(e0 + i)], h_scales[:, cols(e0 + i)])
-
-        def leave(bank, tag):
-            y = keep.tile([P, 2 * C], F32, name="y", tag=tag, align_bytes=64)
-            nc.scalar.copy(out=y[:], in_=bank)
-            return y
-
-        def scatter(e0, half, y):
-            nc.vector.tensor_tensor(
-                windows[half][:].indirect(offsets[:, e0 * C // 16 : (e0 + 2) * C // 16]),
-                y[:],
-                gates[:, cols(e0, 2)],
-                MULT,
-            )
-
-        def operands(e, i):
-            return (x_codes, x_scales, cols(i)) if e == SHARED else (g_codes, g_scales, cols(i))
-
-        positive = {}
-        hidden = {}
-
-        def relu_step(e, i):
-            positive[e, i] = relu_side(e, *operands(e, i), f"positive_{e}_{i}")
-
-        def product_step(e, i):
-            hidden[e, i] = factor_side(e, *operands(e, i), positive[e, i], f"hidden_{e}_{i}")
-
-        def run(chunks):
-            for done, ahead in zip(chunks, chunks[1:]):
-                relu_step(*ahead)
-                product_step(*done)
-
-        def weave_tokens(i, n, tag):
-            return weave(pairs[:], T, i * P, (i + n) * P, tag)
-
-        def quantize_into(source, codes, scales, i, n):
-            quantize(source, codes[:, cols(i, n)], scales[:, cols(i, n)])
-
-        h_codes = keep.tile([P, S], U32, name="h_codes", align_bytes=64)
-        h_scales = keep.tile([P, S], U8, name="h_scales", align_bytes=64)
-        picked = [keep.tile([P, 4 * C], U32, name="picked", tag=f"picked{g}", align_bytes=64) for g in range(2)]
         cast_pairs(nc.vector.tensor_copy, 0, 0, x_low[:])
         cast_pairs(nc.scalar.copy, 1, 0, x_high[0][:])
-        w_routed = keep.tile([P, 2 * E, 2 * H], U8, name="w_routed", tag="x_high0", align_bytes=64)
+        w_routed = sb([P, 2 * E, 2 * H], U8, "w_routed", "x_high0")
         load_words(w_routed[:, :E, :], w1_words[:E])
         load_words(w_routed[:, E:, :], w3_words[:E])
         cast_pairs(nc.scalar.copy, 1, X_SPLIT, x_high[1][:])
-        second = keep.tile([P, (E + 1) * 3 * N], U8, name="second", tag="x_high1", align_bytes=64)
+        second = sb([P, (E + 1) * 3 * N], U8, "second", "x_high1")
         s2 = second[:, : (E + 1) * N].rearrange("p (e c) -> p e c", c=N)
         w2 = second[:, (E + 1) * N :].rearrange("p (e b) -> p e b", b=2 * N)
         load_words(w2, w2_words)
         load_scales(nc.gpsimd, s2, w2_scales)
 
-        first_tokens = weave_tokens(0, 2, "tokens0")
+        first_tokens = weave(pairs[:], T, 0, 2 * P, "tokens0")
         for u in range(2):
             for g in range(2):
-                gather(picked[g], u, g * 2 * C)
-        quantize_into(first_tokens[:], x_codes, x_scales, 0, 2)
-        quantize_into(weave(picked[0][:], 2 * C, 0, 2 * C, "slots0")[:], g_codes, g_scales, 0, 2)
-        later_tokens = weave_tokens(2, 3, "tokens2")
-        quantize_into(later_tokens[:, : 4 * P], x_codes, x_scales, 2, 2)
-        quantize_into(later_tokens[:, 4 * P :], x_codes, x_scales, 4, 1)
-        quantize_into(weave(picked[1][:], 2 * C, 0, 2 * C, "slots1")[:], g_codes, g_scales, 2, 2)
-        gates = keep.tile([P, S], F32, name="gates", tag="slots1", align_bytes=64)
+                gather(g, u)
+        quantize(first_tokens[:], x_codes, x_scales, 0, 2)
+        quantize(weave(picked[0][:], 2 * C, 0, 2 * C, "slots0")[:], g_codes, g_scales, 0, 2)
+        later_tokens = weave(pairs[:], T, 2 * P, T, "tokens2")
+        quantize(later_tokens[:, : 4 * P], x_codes, x_scales, 2, 2)
+        quantize(later_tokens[:, 4 * P :], x_codes, x_scales, 4, 1)
+        quantize(weave(picked[1][:], 2 * C, 0, 2 * C, "slots1")[:], g_codes, g_scales, 2, 2)
+        gates = sb([P, S], F32, "gates", "slots1")
         nc.sync.dma_start(out=gates[:], in_=gate[0:P, :])
-
 
         shared = [(SHARED, i) for i in range(T // P)]
         routed = [(e, e) for e in range(E)]
 
-        def quantize_hidden(chunks, codes, scales, tag):
-            quantize_into(turn([hidden[c] for c in chunks], tag), codes, scales, chunks[0][1], len(chunks))
-
-        relu_step(*shared[0])
-        run(shared[:3] + routed)
-        product_step(*routed[3])
-        quantize_hidden(routed[:2], h_codes, h_scales, "turned_r0")
-        bank = psum.tile([P, 2 * C], F32, name="bank_y", tag="y", bufs=1)
-        routed_products(0, bank, 0, 2)
-        quantize_hidden(routed[2:], h_codes, h_scales, "turned_r2")
-        scatter(0, 0, leave(bank[:], "y_first"))
-        third = psum.tile([P, 2 * C], F32, name="bank_y", tag="y", bufs=1)
-        routed_products(0, third, 2, 2)
-        relu_step(*shared[3])
-        run(shared[3:])
-        product_step(*shared[4])
-        second_bank = psum.tile([P, 2 * C], F32, name="bank_second", tag="sums", bufs=5)
-        routed_products(1, second_bank, 0, 2)
-        slot_gates = keep.tile([P, 2], F32, name="slot_gates", tag="positive_0_0", align_bytes=64)
-        with nc.allow_non_contiguous_dma(reason="one gate value a partition"):
-            nc.sync.dma_start(out=slot_gates[:], in_=gate[0, 2 * C :].rearrange("(j p) -> p j", p=P))
-        slot_major = psum.tile([P, 2, P], F32, name="bank_slots", tag="sums", bufs=5)
-        for j in range(2):
-            nc.tensor.matmul_mx(
-                out=slot_major[:, j, :],
-                lhsT=h_codes[:, cols(2 + j)].bitcast(FP8X4),
-                lhsT_scale=h_scales[:, cols(2 + j)],
-                rhs=w2[:, 2 + j, 2 * P :].bitcast(FP4X4),
-                rhs_scale=s2[:, 2 + j, P:],
-                start=True,
-                stop=True,
-            )
-        quantize_hidden(shared[:2], hs_codes, hs_scales, "positive_4_3")
-        scatter(0, 1, leave(second_bank[:], "positive_4_4"))
-        quantize_hidden(shared[2:4], hs_codes, hs_scales, "turned_s2")
-        by_slot = keep.tile([P, 2, P], F32, name="by_slot")
-        for j in range(2):
-            nc.scalar.activation(by_slot[:, j, :], slot_major[:, j, :], COPY, scale=slot_gates[:, j : j + 1])
-        back = psum.tile([P, 2, P], F32, name="bank_back", tag="sums", bufs=5)
-        for j in range(2):
-            nc.tensor.transpose(back[:, j, :], by_slot[:, j, :], ident[:])
-        quantize_hidden(shared[4:], hs_codes, hs_scales, "turned_s4")
-        scatter(2, 0, leave(third[:], "hidden_4_4"))
-        y_last = leave(back[:].rearrange("p j s -> p (j s)"), "turned_s2")
-        bodies = []
-        for half in range(HALVES):
-            bodies.append(psum.tile([P, 4 * P], F32, name="bank_body", tag="sums", bufs=5))
-            layer2(SHARED, half, bodies[half][:], hs_codes[:, cols(0, 4)], hs_scales[:, cols(0, 4)])
-        tails = psum.tile([P, HALVES, P], F32, name="bank_tails", tag="sums", bufs=5)
-        for half in range(HALVES):
-            layer2(SHARED, half, tails[:, half, :], hs_codes[:, cols(4)], hs_scales[:, cols(4)])
-
-        def finish(engine, half, piece, shared_sums, queue=nc.sync):
-            engine.tensor_tensor(results[half][:, piece], shared_sums, windows[half][:, piece], ADD)
-            queue.dma_start(out=out[half * P : (half + 1) * P, piece], in_=results[half][:, piece])
-
-        nc.vector.tensor_copy(windows[1][:].indirect(offsets[:, 2 * C // 16 :]), y_last[:])
-        results = [keep.tile([P, T], F32, name="result_low")]
-        body_sums = keep.tile([P, 4 * P], F32, name="body_sums", tag="body_sums")
-        nc.scalar.copy(out=body_sums[:], in_=bodies[0][:])
-        tail_sums = keep.tile([P, HALVES, P], F32, name="tail_sums")
-        nc.scalar.copy(out=tail_sums[:], in_=tails[:])
-        finish(nc.gpsimd, 0, cols(0, 4), body_sums[:])
-        results.append(keep.tile([P, T], F32, name="result_high", tag="body_sums"))
-        for half in range(HALVES):
-            finish(nc.gpsimd, half, cols(4), tail_sums[:, half, :])
-        for piece in (slice(0, 320), slice(320, 512)):
-            finish(nc.vector, 1, piece, bodies[1][:, piece], nc.scalar)
+        relu_side(shared[0], 0)
+        relu_side(shared[1], 2)
+        factor_side(shared[0], 1)
+        relu_side(shared[2], 4)
+        factor_side(shared[1], 3)
+        relu_side(routed[0], 6)
+        factor_side(shared[2], 5)
+        relu_side(routed[1], 0)
+        factor_side(routed[0], 7)
+        relu_side(routed[2], 4)
+        factor_side(routed[1], 2)
+        relu_side(routed[3], 6)
+        factor_side(routed[2], 1)
+        factor_side(routed[3], 3)
+        turn_and_quantize(routed[:2], 5)
+        relu_side(shared[3], 0)
+        factor_side(shared[3], 7)
+        turn_and_quantize(routed[2:], 6)
+        relu_side(shared[4], 4)
+        factor_side(shared[4], 2)
+        y_low = leave_low(0, 1)
+        y_high = leave_high(0, 3)
+        turn_and_quantize(shared[:2], 5)
+        scatter_low(0, y_low)
+        turn_and_quantize(shared[2:4], 0)
+        turn_and_quantize(shared[4:], 4)
+        y_low = leave_low(2, 6, "hidden_4_4")
+        scatter_high(0, y_high)
+        y_high = leave_high(2, 7)
+        scatter_low(2, y_low)
+        scatter_high(2, y_high)
+        bodies = [bank(number, [P, 4 * P]) for number in (2, 1)]
+        tails = bank(3, [P, 2, P])
+        for half in range(2):
+            second_layer(SHARED, half, bodies[half][:], hs_codes[:, cols(0, 4)], hs_scales[:, cols(0, 4)])
+        for half in range(2):
+            second_layer(SHARED, half, tails[:, half, :], hs_codes[:, cols(4)], hs_scales[:, cols(4)])
+        finish(0, cols(0, 4), bodies[0][:], nc.sync)
+        finish(0, cols(4), tails[:, 0, :], nc.sync)
+        finish(1, slice(0, 320), bodies[1][:, 0:320], nc.sync)
+        finish(1, slice(320, 512), bodies[1][:, 320:512], nc.scalar)
+        finish(1, cols(4), tails[:, 1, :], nc.sync)

from contextlib import ExitStack

import concourse.mybir as mybir
from concourse.masks import make_identity

FLOPS = 1509949440

K, T, E, C, H, N = 512, 640, 4, 128, 512, 256
S = E * C
SHARED = E
P = 128

F32 = mybir.dt.float32
BF16 = mybir.dt.bfloat16
I32 = mybir.dt.int32
U32 = mybir.dt.uint32
U16 = mybir.dt.uint16
U8 = mybir.dt.uint8
FP8X4 = mybir.dt.float8_e4m3fn_x4
FP4X4 = mybir.dt.float4_e2m1fn_x4
RELU = mybir.ActivationFunctionType.Relu
COPY = mybir.ActivationFunctionType.Copy
MULT = mybir.AluOpType.mult
ADD = mybir.AluOpType.add

X_SPLIT = 256


def tile_moe_shr_glu_relu_kernel(
    tc, xT, w1_words, w1_scales, w3_words, w3_scales, w2_words, w2_scales, gate, offs, out
):
    nc = tc.nc
    with ExitStack() as ctx:
        keep = ctx.enter_context(tc.tile_pool(name="keep", bufs=1))
        psum = ctx.enter_context(tc.psum_pool(name="psum", bufs=1))

        def sb(shape, dtype, name, tag=None):
            return keep.tile(shape, dtype, name=name, tag=tag or name, align_bytes=64)

        def bank(number, shape):
            return psum.tile(shape, F32, name="bank", tag=f"bank{number}")

        def cols(i, n=1):
            return slice(i * P, (i + n) * P)

        offsets = keep.tile([P, S // 16], U16, name="offsets")
        x_low = sb([P, 2, T], F32, "x_low")
        x_high = [sb([P, 2, n], F32, f"x_high{i}") for i, n in enumerate((X_SPLIT, T - X_SPLIT))]
        w_shared = [sb([P, 1, 2 * H], U8, f"w_shared{i}") for i in range(2)]
        s1 = sb([P, E + 1, H], U8, "s1")
        s3 = sb([P, E + 1, H], U8, "s3")
        ident = sb([P, P], F32, "ident")
        pairs = sb([P, 2 * T], U32, "pairs")
        x_codes, x_scales = sb([P, T], U32, "x_codes"), sb([P, T], U8, "x_scales")
        g_codes, g_scales = sb([P, S], U32, "g_codes"), sb([P, S], U8, "g_scales")
        hs_codes, hs_scales = sb([P, T], U32, "hs_codes"), sb([P, T], U8, "hs_scales")
        h_codes, h_scales = sb([P, S], U32, "h_codes"), sb([P, S], U8, "h_scales")
        picked = [sb([P, 4 * C], U32, f"picked{g}") for g in range(2)]
        windows = [sb([P, T], F32, f"window{half}") for half in range(2)]
        results = [sb([P, T], F32, f"result{half}") for half in range(2)]

        x_rows = xT.rearrange("(p j) t -> p j t", j=4)

        def load_words(tile, words):
            nc.sync.dma_start(out=tile.bitcast(I32), in_=words[:, 0].rearrange("e p b -> p e b").bitcast(I32))

        def load_scales(engine, tile, scales):
            engine.memset(tile.rearrange("p e c -> p (e c)").bitcast(I32), 0)
            rows = scales[:, 0].rearrange("e (q r) c -> r q e c", r=4)
            for r in range(4):
                nc.sync.dma_start(out=tile[r:P:32, :, :].bitcast(I32), in_=rows[r].bitcast(I32))

        def cast_pairs(copy, u, t0, rows):
            t1 = t0 + rows.shape[2]
            copy(
                out=pairs[:, u * T + t0 : u * T + t1].bitcast(BF16).rearrange("p (t d) -> p t d", d=2),
                in_=rows.rearrange("p d t -> p t d"),
            )

        def weave(planes, width, t0, t1, name):
            woven = sb([P, 2 * (t1 - t0)], U32, name)
            nc.scalar.copy(
                out=woven[:].rearrange("p (t u) -> p t u", u=2),
                in_=planes.rearrange("p (u t) -> p t u", t=width)[:, t0:t1, :],
            )
            return woven

        def quantize(words, codes, scales, i, n):
            nc.vector.quantize_mx(out=codes[:, cols(i, n)].bitcast(FP8X4), scales=scales[:, cols(i, n)], in_=words.bitcast(BF16))

        def listed(j0, n):
            return offsets[:, j0 // 16 : (j0 + n) // 16]

        def gather(g, u):
            nc.vector.tensor_copy(
                out=picked[g][:, u * 2 * C : (u + 1) * 2 * C],
                in_=pairs[:, u * T : (u + 1) * T].indirect(listed(g * 2 * C, 2 * C)),
            )

        def product(sums, lhsT, lhsT_scale, rhs, rhs_scale):
            nc.tensor.matmul_mx(out=sums, lhsT=lhsT, lhsT_scale=lhsT_scale, rhs=rhs, rhs_scale=rhs_scale, start=True, stop=True)

        def first_layer(chunk, side, number):
            e, i = chunk
            codes, scales = (x_codes, x_scales) if e == SHARED else (g_codes, g_scales)
            words = w_shared[side][:, 0, :] if e == SHARED else w_routed[:, side * E + e, :]
            sums = bank(number, [P, H])
            product(sums[:], codes[:, cols(i)].bitcast(FP8X4), scales[:, cols(i)], words.bitcast(FP4X4), (s1, s3)[side][:, e, :])
            return sums

        def in_pairs(ap, pattern):
            return ap.rearrange(pattern, u=2, d=2)

        positive = {}
        hidden = {}

        def relu_side(chunk, number):
            sums = first_layer(chunk, 0, number)
            positive[chunk] = sb([P, H], F32, "positive_%d_%d" % chunk)
            nc.scalar.activation(in_pairs(positive[chunk][:], "p (u r d) -> p u r d"), in_pairs(sums[:], "p (r u d) -> p u r d"), RELU)

        def factor_side(chunk, number):
            sums = first_layer(chunk, 1, number)
            hidden[chunk] = sb([P, H], BF16, "hidden_%d_%d" % chunk)
            nc.vector.tensor_tensor(
                in_pairs(hidden[chunk][:], "p (u r d) -> p u r d"),
                in_pairs(sums[:], "p (r u d) -> p u r d"),
                in_pairs(positive[chunk][:], "p (u r d) -> p u r d"),
                MULT,
            )

        def turn_and_quantize(chunks, number):
            e, i = chunks[0]
            n = len(chunks)
            turned_sums = bank(number, [P, n, 2, P])
            for j, chunk in enumerate(chunks):
                words = hidden[chunk][:].bitcast(F32)
                for u in range(2):
                    nc.tensor.transpose(turned_sums[:, j, u, :], words[:, cols(u)], ident[:])
            turned = sb([P, n, P, 2], F32, "turned_%d_%d" % chunks[0])
            nc.scalar.copy(out=turned[:], in_=turned_sums[:].rearrange("p i u r -> p i r u"))
            codes, scales = (hs_codes, hs_scales) if e == SHARED else (h_codes, h_scales)
            quantize(turned[:].rearrange("p i r u -> p (i r u)"), codes, scales, i, n)

        def second_layer(e, half, sums, codes, scales):
            product(sums, w2[:, e, 2 * P * half : 2 * P * (half + 1)].bitcast(FP4X4), s2[:, e, cols(half)], codes.bitcast(FP8X4), scales)

        def routed_sums(e0, half, number):
            sums = bank(number, [P, 2 * C])
            for j in range(2):
                second_layer(e0 + j, half, sums[:, cols(j)], h_codes[:, cols(e0 + j)], h_scales[:, cols(e0 + j)])
            return sums

        def leave_low(e0, number, tag=None):
            sums = routed_sums(e0, 0, number)
            y = sb([P, 2 * C], F32, f"y_low{e0}", tag)
            nc.scalar.copy(out=y[:], in_=sums[:])
            return y

        def leave_high(e0, number):
            sums = routed_sums(e0, 1, number)
            y = sb([P, 2 * C], F32, f"y_high{e0}")
            nc.vector.tensor_tensor(y[:], sums[:], gates[:, cols(e0, 2)], MULT)
            return y

        def scatter_low(e0, y):
            nc.vector.tensor_tensor(windows[0][:].indirect(listed(e0 * C, 2 * C)), y[:], gates[:, cols(e0, 2)], MULT)

        def scatter_high(e0, y):
            nc.scalar.activation(windows[1][:].indirect(listed(e0 * C, 2 * C)), y[:], COPY)

        def finish(half, piece, shared_sums, queue):
            nc.vector.tensor_tensor(results[half][:, piece], shared_sums, windows[half][:, piece], ADD)
            queue.dma_start(out=out[cols(half), piece], in_=results[half][:, piece])

        nc.sync.dma_start(out=x_low[:], in_=x_rows[:, 0:2, :])
        nc.sync.dma_start(offsets[:], offs)
        nc.sync.dma_start(out=x_high[0][:], in_=x_rows[:, 2:4, :X_SPLIT])
        nc.sync.dma_start(out=x_high[1][:], in_=x_rows[:, 2:4, X_SPLIT:])
        load_words(w_shared[0][:], w1_words[SHARED:])
        load_words(w_shared[1][:], w3_words[SHARED:])
        load_scales(nc.gpsimd, s1[:], w1_scales)
        load_scales(nc.vector, s3[:], w3_scales)
        nc.vector.memset(windows[0][:], 0.0)
        make_identity(nc, ident[:])
        nc.scalar.activation(windows[1][:], windows[0][:], RELU)

        cast_pairs(nc.vector.tensor_copy, 0, 0, x_low[:])
        cast_pairs(nc.scalar.copy, 1, 0, x_high[0][:])
        w_routed = sb([P, 2 * E, 2 * H], U8, "w_routed", "x_high0")
        load_words(w_routed[:, :E, :], w1_words[:E])
        load_words(w_routed[:, E:, :], w3_words[:E])
        cast_pairs(nc.scalar.copy, 1, X_SPLIT, x_high[1][:])
        second = sb([P, (E + 1) * 3 * N], U8, "second", "x_high1")
        s2 = second[:, : (E + 1) * N].rearrange("p (e c) -> p e c", c=N)
        w2 = second[:, (E + 1) * N :].rearrange("p (e b) -> p e b", b=2 * N)
        load_words(w2, w2_words)
        load_scales(nc.gpsimd, s2, w2_scales)

        first_tokens = weave(pairs[:], T, 0, 2 * P, "tokens0")
        for u in range(2):
            for g in range(2):
                gather(g, u)
        quantize(first_tokens[:], x_codes, x_scales, 0, 2)
        quantize(weave(picked[0][:], 2 * C, 0, 2 * C, "slots0")[:], g_codes, g_scales, 0, 2)
        later_tokens = weave(pairs[:], T, 2 * P, T, "tokens2")
        quantize(later_tokens[:, : 4 * P], x_codes, x_scales, 2, 2)
        quantize(later_tokens[:, 4 * P :], x_codes, x_scales, 4, 1)
        quantize(weave(picked[1][:], 2 * C, 0, 2 * C, "slots1")[:], g_codes, g_scales, 2, 2)
        gates = sb([P, S], F32, "gates", "slots1")
        nc.sync.dma_start(out=gates[:], in_=gate[0:P, :])

        shared = [(SHARED, i) for i in range(T // P)]
        routed = [(e, e) for e in range(E)]

        relu_side(shared[0], 0)
        relu_side(shared[1], 2)
        factor_side(shared[0], 1)
        relu_side(shared[2], 4)
        factor_side(shared[1], 3)
        relu_side(routed[0], 6)
        factor_side(shared[2], 5)
        relu_side(routed[1], 0)
        factor_side(routed[0], 7)
        relu_side(routed[2], 4)
        factor_side(routed[1], 2)
        relu_side(routed[3], 6)
        factor_side(routed[2], 1)
        factor_side(routed[3], 3)
        turn_and_quantize(routed[:2], 5)
        relu_side(shared[3], 0)
        factor_side(shared[3], 7)
        turn_and_quantize(routed[2:], 6)
        relu_side(shared[4], 4)
        factor_side(shared[4], 2)
        y_low = leave_low(0, 1)
        y_high = leave_high(0, 3)
        turn_and_quantize(shared[:2], 5)
        scatter_low(0, y_low)
        turn_and_quantize(shared[2:4], 0)
        turn_and_quantize(shared[4:], 4)
        y_low = leave_low(2, 6, "hidden_4_4")
        scatter_high(0, y_high)
        y_high = leave_high(2, 7)
        scatter_low(2, y_low)
        scatter_high(2, y_high)
        bodies = [bank(number, [P, 4 * P]) for number in (2, 1)]
        tails = bank(3, [P, 2, P])
        for half in range(2):
            second_layer(SHARED, half, bodies[half][:], hs_codes[:, cols(0, 4)], hs_scales[:, cols(0, 4)])
        for half in range(2):
            second_layer(SHARED, half, tails[:, half, :], hs_codes[:, cols(4)], hs_scales[:, cols(4)])
        finish(0, cols(0, 4), bodies[0][:], nc.sync)
        finish(0, cols(4), tails[:, 0, :], nc.sync)
        finish(1, slice(0, 320), bodies[1][:, 0:320], nc.sync)
        finish(1, slice(320, 512), bodies[1][:, 320:512], nc.scalar)
        finish(1, cols(4), tails[:, 1, :], nc.sync)
